import numpy as np, ml_dtypes
CORES = [8,136,40,168]
N = 4
BF = ml_dtypes.bfloat16
def f(rng, *shape):
    return (rng.standard_normal(shape, dtype=np.float32) * np.exp2(rng.integers(-2, 3, shape[:-1] + (1,)))).astype(BF)
def wide(rng, *shape):
    v = f(rng, *shape).astype(np.float32); k = shape[:-2] + (1, shape[-1])
    return (v * np.exp2(rng.integers(-6, 7, k)) * (rng.random(k) > 0.0625)).astype(BF)
def gentries(a):
    return np.ascontiguousarray(a.reshape(8, 16, -1).transpose(0, 2, 1)).reshape(8, -1)
def gtable(e):
    e = np.asarray(e); return np.ascontiguousarray(e.reshape(8, -1, 16).transpose(0, 2, 1)).reshape(128, -1).astype(np.int32)
M, I, Q, W = 3072, 64, 768, 1048576
CAPT, CAP = 127, 256
def parts(rng, n, lo, hi):
    room = rng.permutation(np.repeat(np.arange(len(lo)), hi - lo))[:n - int(np.sum(lo))]
    return lo + np.bincount(room, minlength=len(lo))
def ticks(rng, kind=""):
    times = np.zeros((N, 8, M), np.int32); own = np.zeros((N, 8, M), np.int64)
    for s in range(N):
        for g in range(8):
            lo = rng.integers(0, (M - 2 * CAPT) // I + 1, I); hi = np.full(I, CAPT, np.int64); o = rng.permutation(I)
            if kind == "full":
                lo[:] = 0; lo[o[:M // CAPT]] = CAPT
            else:
                c, z = o[:2], o[2:2 + I // 16]
                if kind == "ends":
                    c, z = (np.array([0, I - 1]), o[:0]) if s % 2 == 0 else (o[:0], np.array([0, I - 1]))
                lo[c] = CAPT; lo[z] = 0; hi[z] = 0
            own[s, g] = rng.permutation(np.repeat(np.arange(I), parts(rng, M, lo, hi)))
            t = rng.integers(0, W, M); t = np.where(rng.random(M) < 0.5, t, t - t % (W // 64))
            if kind == "ties":
                t = np.concatenate([[0, W - 1], rng.integers(0, W, 14)])[rng.integers(0, 16, M)]
            if kind == "ends":
                if rng.random() < 0.5:
                    t[0] = 0; t[1] = W - 1
                else:
                    t = W // 4 + t // 2
            times[s, g] = s * W + np.sort(t)
    return times, own
def index(own):
    pm = np.stack([gtable(np.argsort(own[s], axis=1, kind="stable")) for s in range(N)])
    starts = np.zeros((N, 8, I + 1), np.int32)
    for s in range(N):
        for g in range(8):
            starts[s, g, 1:] = np.add.accumulate(np.bincount(own[s, g], minlength=I))
    return pm, starts
def queries(rng, times, own, full=False):
    qi = np.zeros((N, 8, Q), np.int32); qt = np.zeros((N, 8, Q), np.int32)
    for r in range(N):
        a, b = rng.choice(8, 2, replace=False)
        for g in range(8):
            lo = np.zeros(N, np.int64); hi = np.full(N, CAP, np.int64); o = (r + 1 + rng.permutation(N - 1)) % N
            if full:
                if g % 2 == 1:
                    o = np.concatenate([[r], o])
                lo[o[:Q // CAP]] = CAP
            elif g == a:
                lo[o[0]] = CAP
            elif g == b:
                hi[o[0]] = 0
            s = rng.permutation(np.repeat(np.arange(N), parts(rng, Q, lo, hi)))
            k = rng.integers(0, M, Q); u = rng.random(Q)
            i = np.where(u < 0.5, own[s, g, k], rng.integers(0, I, Q))
            t = np.where((u > 0.25) & (u < 0.75), times[s, g, k], s * W + rng.integers(0, W, Q))
            t = np.where((u > 0.4) & (u < 0.5), np.maximum(t - 1, s * W), t)
            qi[r, g] = i; qt[r, g] = t
    return qi, qt
def sparse(rng, v):
    keep = rng.random((N, 128, M), dtype=np.float32) < np.exp2(-rng.integers(1, 7, (N, 128, 1)))
    return np.where(keep, v.astype(np.float32), np.float32(0)).astype(BF)
def make(rng, kind=""):
    times, own = ticks(rng, kind); pm, starts = index(own); qi, qt = queries(rng, times, own, kind == "full")
    return {"x": sparse(rng, f(rng, N, 128, M)), "times": times, "pm": pm, "starts": starts, "qi": qi, "qt": qt}
def setup_inputs(rng):
    return make(rng)
def setup_inputs_ends(rng):
    d = make(rng, "ends"); qt = d["qt"].astype(np.int64); s = qt // W; g = np.arange(8)[None, :, None]
    first = d["times"][s, g, 0].astype(np.int64); last = d["times"][s, g, M - 1].astype(np.int64)
    c = rng.integers(0, 6, qt.shape)
    t = np.choose(c, [s * W, s * W + W - 1, np.maximum(first - 1, s * W), np.minimum(last + 1, s * W + W - 1), last, qt])
    e = rng.random(qt.shape)
    d["qi"] = np.where(e < 0.25, 0, np.where(e < 0.5, I - 1, d["qi"])).astype(np.int32); d["qt"] = t.astype(np.int32); return d
def setup_inputs_full(rng):
    return make(rng, "full")
def setup_inputs_ties(rng):
    return make(rng, "ties")
def setup_inputs_old(rng):
    d = make(rng); h = np.where(rng.random(128) < 0.5, 0, rng.integers(0, N, 128))
    keep = (np.arange(N)[:, None] == h)[:, :, None] & (rng.random((N, 128, M), dtype=np.float32) < 0.25)
    d["x"] = np.where(keep, f(rng, N, 128, M).astype(np.float32), np.float32(0)).astype(BF); return d
def setup_inputs_spread(rng):
    d = make(rng); d["x"] = sparse(rng, wide(rng, N, 128, M)); return d
def check_inputs(d):
    bad = []; t = d["times"].astype(np.int64); st = d["starts"].astype(np.int64); qi = d["qi"]; qt = d["qt"].astype(np.int64)
    e = np.stack([gentries(a) for a in d["pm"]]).astype(np.int64); s0 = (np.arange(N) * W)[:, None, None]
    size = np.abs(d["x"].astype(np.float32))
    if not np.isfinite(size).all(): bad.append("x finite")
    if not ((size == 0) | (size >= 2.0 ** -100)).all(): bad.append("x size")
    if not ((t >= s0) & (t < s0 + W)).all(): bad.append("times in the slice")
    if not (np.diff(t, axis=2) >= 0).all(): bad.append("times in order")
    n = np.diff(st, axis=2)
    if not ((st[:, :, 0] == 0).all() and (st[:, :, I] == M).all() and (n >= 0).all()): bad.append("starts")
    else:
        if not (n <= CAPT).all(): bad.append("ticks of an instrument")
        for s in range(N):
            for g in range(8):
                edge = np.zeros(M + 1, bool); edge[st[s, g]] = True
                if not ((np.diff(e[s, g]) > 0) | edge[1:M]).all() and "pm in order" not in bad: bad.append("pm in order")
    if not (np.sort(e, axis=2) == np.arange(M)).all(): bad.append("pm a permutation")
    if not ((qi >= 0) & (qi < I)).all(): bad.append("qi range")
    if not ((qt >= 0) & (qt < N * W)).all(): bad.append("qt range")
    if not all((np.sum(qt // W == s, axis=2) <= CAP).all() for s in range(N)): bad.append("queries in a slice")
    return bad
def reference(x, times, pm, starts, qi, qt):
    y = np.zeros((N, 8, 16, Q), np.float32)
    for g in range(8):
        i = qi[:, g].reshape(-1).astype(np.int64); key = i * (N * W) + qt[:, g].reshape(-1)
        v = np.zeros((16, N * Q), np.float32)
        for s in range(N):
            e = gentries(pm[s])[g]; st = starts[s, g].astype(np.int64)
            w = x[s, 16 * g:16 * g + 16].astype(np.float32)[:, e]
            p = np.searchsorted(np.repeat(np.arange(I), np.diff(st)) * (N * W) + times[s, g][e], key, "right")
            last = np.maximum.accumulate(np.where(w != 0, np.arange(M), -1), axis=1)
            last = np.concatenate([np.full((16, 1), -1, np.int64), last], axis=1)[:, p]
            v = np.where(last >= st[i], np.take_along_axis(w, np.maximum(last, 0), axis=1), v)
        y[:, g] = v.reshape(16, N, Q).transpose(1, 0, 2)
    return {"y": y.reshape(N, 128, Q).astype(BF)}

@@ -1,0 +1,404 @@
+from concourse.mybir import AluOpType as A, AxisListType, ActivationFunctionType as AF
+
+M, NI, Q, CAP = 3072, 64, 768, 256
+BL = CAP + NI
+BIG = float(2 ** 23)
+F32, BF, I32, U16 = "float32", "bfloat16", "int32", "uint16"
+_S = {
+    BF: dict(X=M, XS=M, Z=M + 512, F=M + 16, TW=M, TS=M + 144, TP=576, QP=192, QR=Q, QW=4 * BL, QL=3 * CAP, E=192,
+             RST=192, ONE=128, CR=192, C16=128, CM16=128, TMPA=128, TMPB=128, TMPC=128, CW=32, BLK=[8, 16], TRI=128,
+             BLKP=[8, 16], B3=[3, 8, 16], WS=720, OH=192, XE=192, G1=576, CMP=4 * CAP, CMQ=4 * CAP, ANS=3 * BL,
+             AL=4 * BL, CT=256, CZ=128, CY=64, AG=Q, MZ=Q, TT=Q, YB=Q),
+    F32: dict(QF=48, QF2=48, QT=4 * CAP, CN=192, CN2=192, CN3=96, PC=[6, 16], TI=[6, 2, 16], TO=[6, 2, 16], R=[6, 16],
+              KC=24, IO=192, GR=16, TWO=8, GT=16, I9=9, PB=9, D=4, SF=8, SM=32, XT=16, P2L=36, PENA=64, PEN=576,
+              PLO=64, L2=208, AT=64, P2=576),
+    I32: dict(PM=192, TB=192, TI3=576, QB=96, QI3=144, QS=48, QH=48, IP=4, I12=12, SE=8, C0=4, WI=64, WJ=64),
+    U16: dict(PMU=192, POS=96, U12=12, P2U=36, G1U=36, RU=4, O1=64, O2=64, O3=80),
+}
+SCRATCH = {_n: ("sbuf", [128] + (_c if isinstance(_c, list) else [_c]), _d) for _d in _S for _n, _c in _S[_d].items()}
+for _b in range(8):
+    SCRATCH["ps%d" % _b] = ("psum", [128, 512], F32)
+
+SEMAPHORES = ["V", "S", "P", "G", "sent", "q0", "q1", "q2", "ans"] + ["d%d" % _i for _i in range(24)]
+
+
+def rank_program(g, core, T, topo):
+    rank = T.rank_of(core)
+    if rank is None:
+        return
+    N = len(T.cores)
+    queue = {"V": g.vector, "S": g.scalar, "P": g.tensor, "G": g, "Y": g.sync}
+    V, S, P = g.vector, g.scalar, g.tensor
+    ops, state, ndma, nsent = [], {}, [0], [0]
+
+    def op(eng, fn, r="", w="", dma=False):
+        me = {"eng": eng, "fn": fn, "deps": [], "dma": None, "used": False, "ext": None}
+        if dma:
+            me["dma"] = "d%d" % ndma[0]
+            ndma[0] += 1
+        for k in r.split():
+            st = state.setdefault(k, {"w": None, "r": []})
+            if st["w"] is not None:
+                me["deps"].append(st["w"])
+            if k.startswith("ps"):
+                me["deps"] += [o for o in st["r"] if o["eng"] != eng]
+        for k in w.split():
+            st = state.setdefault(k, {"w": None, "r": []})
+            for o in ([st["w"]] if st["w"] is not None else []) + st["r"]:
+                if not (eng == "P" and o["eng"] == "P"):
+                    me["deps"].append(o)
+        for k in r.split():
+            state[k]["r"].append(me)
+        for k in w.split():
+            state[k] = {"w": me, "r": []}
+        for o in me["deps"]:
+            o["used"] = True
+        ops.append(me)
+
+    def landing(key, sem, val):
+        state[key] = {"w": {"eng": None, "dma": None, "ext": (sem, val), "used": True}, "r": []}
+
+    def ts(out, in0, s1, s2, op0, op1, r, w):
+        if op1 is None:
+            op("V", lambda: V.tensor_scalar(out, in0, s1, None, op0), r, w)
+        else:
+            op("V", lambda: V.tensor_scalar(out, in0, s1, s2, op0, op1), r, w)
+
+    def t1(out, in0, s1, op0, r, w):
+        ts(out, in0, s1, None, op0, None, r, w)
+
+    def tt(out, in0, in1, o, r, w):
+        op("V", lambda: V.tensor_tensor(out, in0, in1, o), r, w)
+
+    def cp(out, in_, r, w):
+        op("V", lambda: V.tensor_copy(out, in_), r, w)
+
+    def ms(ap, c, w):
+        op("V", lambda: V.memset(ap, c), "", w)
+
+    def scan(out, d0, d1, init, op1, r, w):
+        op("V", lambda: V.tensor_tensor_scan(out, d0, d1, init, A.mult, op1), r, w)
+
+    def act(out, in_, f, r, w, **kw):
+        op("S", lambda: S.activation(out, in_, f, **kw), r, w)
+
+    def move(eng, out, in_, r, w):
+        if eng == "S":
+            act(out, in_, AF.Copy, r, w)
+        else:
+            cp(out, in_, r, w)
+
+    def mm(items, r, w):
+        def fn():
+            last = None
+            for (o, l, rh, st, sp) in items:
+                last = P.matmul(o, l, rh, st, sp)
+            return last
+        op("P", fn, r, w)
+
+    def dma(eng, out, in_, r, w):
+        op(eng, lambda: queue[eng].dma_start(out, in_), r, w, dma=True)
+
+    def iota(out, pattern, base, cm, w, flag=True):
+        if flag:
+            op("G", lambda: g.iota(out, pattern, base, cm, allow_small_or_imprecise_dtypes=True), "", w)
+        else:
+            op("G", lambda: g.iota(out, pattern, base, cm), "", w)
+
+    def sel(out, in_, pattern, cmp, base, cm, r, w):
+        op("G", lambda: g.affine_select(out, in_, pattern, cmp, 0.0, base, cm), r, w)
+
+    def send(dst_rank, out, in_, sem, r):
+        dst = T.cores[dst_rank]
+        rid, pid = topo.addr(dst, core)
+        mask = topo.mask(core, dst)
+        nsent[0] += len(topo.engines(core, dst))
+        op("G", lambda: g.remote_dma(out, in_, T.sem[sem], T.sem.sent, pid, rid, mask), r, "")
+
+    ps = [T["ps%d" % b] for b in range(8)]
+    KC = T.KC
+    col = lambda j: KC[:, j:j + 1]
+    cK, cD1, cD0, cWB, cPW, cSC, cS0, cBA, cNK, cM7, cT1, cT2 = range(12)
+
+    def slide(x, m):
+        return T.WS[:, 144 * x + 15 - m:144 * x + 143 - m]
+    WP, WI_, WA, WB, W1 = range(5)
+    wcol = lambda x: T.WS[:, 144 * x + 15:144 * x + 143:16]
+
+    def sums(b, c0, x, src, lo, hi, start, stop, r):
+        out = ps[b][:, c0:c0 + (hi - lo) // 16]
+        mm([(out, slide(x, m), src[:, lo + m:hi:16], start and m == 0, stop and m == 15) for m in range(16)],
+           "WS%d %s" % (x, r), "ps%d" % b)
+
+    others = [(rank + 1 + b) % N for b in range(N - 1)]
+    for b in range(N - 1):
+        landing("QL%d" % b, "q%d" % b, len(topo.engines(T.cores[others[b]], core)))
+    landing("ALr", "ans", sum(len(topo.engines(T.cores[o], core)) for o in others))
+
+    dma("Y", T.QB[:, 0:48], T.qt[:], "", "QBt")
+    dma("S", T.QB[:, 48:96], T.qi[:], "", "QBi")
+    dma("Y", T.TB[:], T.times[:], "", "TB")
+    dma("S", T.PM[:], T.pm[:], "", "PM")
+    dma("Y", T.X[:], T.x[:], "", "X")
+    dma("S", T.SE[:, 0:4], T.starts[:, 0:64], "", "SEs")
+    dma("S", T.SE[:, 4:8], T.starts[:, 1:65], "", "SEe")
+
+    ms(T.C16[:], 1.0 / 16, "C16")
+    ms(T.CM16[:], -1.0 / 16, "CM16")
+    ms(T.QW[:], 0.0, "QW")
+    ms(T.ONE[:], 1.0, "ONE")
+    iota(T.IP[:, 0:1], [[0, 1]], 0, 1, "IP0", False)
+    iota(T.IO[:], [[0, 12], [1, 16]], 0, 0, "IO")
+    iota(T.I9[:], [[1, 9]], 0, 0, "I9")
+    grp, neg = [[-16, 8], [0, 16]], [[16, 8], [0, 16]]
+    sel(T.TMPA[:], T.C16[:], grp, A.is_ge, 0, 1, "C16", "TMPA")
+    sel(T.TMPB[:], T.CM16[:], [[-16, 8], [-1, 16]], A.is_gt, 0, 1, "CM16", "TMPB")
+    sel(T.BLK[:], T.TMPA[:], neg, A.is_ge, 15, -1, "TMPA", "BLK")
+    sel(T.TRI[:], T.TMPB[:], neg, A.is_ge, 15, -1, "TMPB", "TRI")
+    iota(T.CR[0:1, :], [[BL // 16, 4], [0, 48]], 0, 0, "CR")
+    iota(T.I12[:], [[1, 12]], 0, 0, "I12", False)
+    iota(T.D[:], [[1, 4]], M, 4, "D")
+    iota(T.WS[:], [[0, 720]], 0, 0, "WSz")
+    iota(T.CW[:, 0:16], [[48, 2], [0, 8]], 16, 0, "CW")
+    sel(T.TMPC[:], T.ONE[:], grp, A.is_ge, 0, 1, "ONE", "TMPC")
+    sel(T.CW[:, 16:24], T.CW[:, 8:16], [[-16, 8]], A.is_ge, 0, 1, "CW", "CWb")
+    sel(T.BLKP[:], T.TMPC[:], neg, A.is_ge, 2, -1, "TMPC", "BLKP")
+    sel(wcol(WP), T.TMPC[:, 0:128:16], [[16, 8]], A.is_ge, 2, -1, "TMPC WSz", "WS0")
+    sel(wcol(WI_), T.CW[:, 0:8], [[-16, 8]], A.is_equal, -3, 1, "CW WSz", "WS1")
+    sel(wcol(WA), T.CW[:, 16:24], [[16, 8]], A.is_ge, 7, -1, "CWb WSz", "WS2")
+    sel(wcol(W1), T.TMPC[:, 0:128:16], [[16, 8]], A.is_ge, 15, -1, "TMPC WSz", "WS4")
+    iota(T.B3[:], [[0, 384]], 0, 0, "B3z")
+    iota(T.TS[:, M:M + 144], [[0, 144]], 0, 0, "TSz")
+    iota(T.CT[:, 0:64], [[0, 64]], 0, 0, "CT0")
+    iota(T.F[:, 0:16], [[0, 16]], 0, 0, "Fz")
+    iota(T.L2[:, 192:208], [[0, 16]], 0, 0, "L2z")
+    move("S", T.QR[:], T.QW[:, 0:Q], "QW", "QRz")
+    for h in range(3):
+        move("S", T.TW[:, 1024 * h:1024 * h + 1024], T.QW[:, 0:1024], "QW", "TWz%d" % h)
+    ms(T.RST[:], 1.0, "RST")
+    ms(T.TWO[:], 2.0, "TWO")
+    t1(T.IP[:, 1:2], T.IP[:, 0:1], 15, A.bitwise_and, "IP0", "IP1")
+    ts(T.IP[:, 2:3], T.IP[:, 0:1], 4, 1, A.arith_shift_right, A.bitwise_and, "IP0", "IP2")
+    ms(T.GR[:, 0:8], 512.0, "GRa")
+    ms(T.RST[:, 0:192:48], 0.0, "RST")
+    cp(KC[:, 0:2], T.IP[:, 1:3], "IP1 IP2", "cK")
+    scan(T.GR[:, 8:16], T.TWO[:], T.TWO[:], 1.0, A.max, "TWO", "GRb")
+    ts(T.OH[:], T.IO[:], col(cK), 16.0, A.is_equal, A.mult, "IO cK", "OH")
+    ts(col(cD0), col(cD1), -1.0, 1.0, A.mult, A.add, "cK", "cD0")
+    t1(col(cM7), col(cK), 7.0, A.is_le, "cK", "cM7")
+    ts(col(cT1), col(cK), -1.0 / 16, 239.0 / 256, A.mult, A.add, "cK", "cT1")
+    tt(T.GT[:], T.GR[:], T.OH[:, 0:16], A.mult, "GRa GRb OH", "GT")
+    ts(T.PB[:], T.I9[:], 16.0, col(cK), A.mult, A.add, "I9 cK", "PB")
+    t1(col(cNK), col(cK), -BIG, A.mult, "cK", "cNK")
+    op("V", lambda: V.tensor_reduce(col(cPW), T.GT[:], AxisListType.X, A.add), "GT", "cPW")
+    ts(col(cBA), col(cT1), col(cM7), -0.5 + 1.0 / 512, A.mult, A.add, "cT1 cM7", "cBA")
+    t1(col(cT2), col(cM7), -65280.0, A.mult, "cM7", "cT2")
+    op("V", lambda: V.reciprocal(col(cS0), col(cPW)), "cPW", "cS0")
+    ts(T.PB[:], T.PB[:], 1.0, BIG, A.add, A.mult, "PB", "PB")
+
+    masks = (0x3F8000, 0x7F80, 0x7F)
+    for j in range(3):
+        t1(T.QI3[:, 48 * j:48 * j + 48], T.QB[:, 0:48], masks[j], A.bitwise_and, "QBt", "QI%d" % j)
+    t1(T.QS[:], T.QB[:, 0:48], 20, A.arith_shift_right, "QBt", "QS")
+    t1(T.QH[:], T.QB[:, 48:96], 2, A.arith_shift_right, "QBi", "QH")
+    cp(T.QP[:, 0:144], T.QI3[:], "QI0 QI1 QI2", "QP")
+    t1(T.QF[:], T.QH[:], -63.0 / 16, A.mult, "QH", "QF")
+    for s in range(N):
+        t1(T.E[:, 48 * s:48 * s + 48], T.QS[:], float(s), A.is_equal, "QS", "E%d" % s)
+        if s == 0:
+            tt(T.QP[:, 144:192], T.QB[:, 48:96], T.QF[:], A.add, "QBi QF", "QP3")
+    for j in range(3):
+        dma("Y", T.QR[j:128:16, :], T.QP[:, 48 * j:48 * j + 48], "QP QRz", "QR%d" % j)
+    dma("Y", T.QR[3:128:16, :], T.QP[:, 144:192], "QP3 QRz", "QR3")
+    Es = "E0 E1 E2 E3"
+    mm([(ps[0][:, 0:192], T.BLK[:], T.E[:], True, True)], "BLK " + Es, "ps0")
+    mm([(ps[1][:, 0:192], T.TRI[:], T.E[:], True, False),
+        (ps[1][:, 0:192], T.ONE[0:1, :], T.CR[0:1, :], False, True)], "TRI ONE CR " + Es, "ps1")
+    for j in range(3):
+        t1(T.TI3[:, 192 * j:192 * j + 192], T.TB[:], masks[j], A.bitwise_and, "TB", "TI%d" % j)
+    scan(T.CN[:], T.RST[:], ps[0][:, 0:192], 0.0, A.add, "RST ps0", "CN")
+    cp(T.TP[:], T.TI3[:], "TI0 TI1 TI2", "TP")
+    for j in range(3):
+        dma("Y", T.TW[j:128:16, :], T.TP[:, 192 * j:192 * j + 192], "TP TWz0 TWz1 TWz2", "TW%d" % j)
+    tt(T.CN2[:], T.CN[:], ps[1][:, 0:192], A.add, "CN ps1", "CN2")
+    ts(T.QF2[:], T.QS[:], 4.0, 1.0 / 16, A.mult, A.add, "QS", "QF2")
+    tt(T.CN[:], T.CN2[:], T.E[:], A.mult, "CN2 " + Es, "CN")
+    tt(T.PC[:, 3:6, :], T.QF2[:], T.QP[:, 144:192], A.add, "QF2 QP3", "PC1")
+    tt(T.CN3[:], T.CN[:, 0:96], T.CN[:, 96:192], A.add, "CN", "CN3")
+    cp(T.PMU[:], T.PM[:], "PM", "PMU")
+    tt(T.PC[:, 0:3, :], T.CN3[:, 0:48], T.CN3[:, 48:96], A.add, "CN3", "PC0")
+    ts(col(cWB), col(cPW), 8.0, col(cT2), A.mult, A.add, "cPW cT2", "cWB")
+    t1(T.TI[:, :, 0, :], T.PC[:], col(cD0), A.mult, "PC0 PC1 cD0", "TIa")
+    t1(T.TI[:, :, 1, :], T.PC[:], col(cD1), A.mult, "PC0 PC1 cK", "TIb")
+    t1(col(cSC), col(cS0), 16.0, A.mult, "cS0", "cSC")
+    op("V", lambda: V.transpose(T.TO[:], T.TI[:]), "TIa TIb", "TO")
+    cp(T.U12[:], T.I12[:], "I12", "U12")
+    tt(T.R[:], T.TO[:, :, 0, :], T.TO[:, :, 1, :], A.add, "TO", "R")
+    cp(T.SF[:], T.SE[:], "SEs SEe", "SF")
+    for u in range(3):
+        ts(T.POS[:, u:96:3], T.R[:, u:6:3, :], 16.0, -1.0, A.mult, A.add, "R", "POS%d" % u)
+    POS = "POS0 POS1 POS2"
+    t1(T.C0[:], T.SE[:, 0:4], 4, A.arith_shift_right, "SEs", "C0")
+    cp(T.QW[:, :].indirect(T.POS[:, 0:48]), T.QR[:], POS + " QR0 QR1 QR2 QR3", "QW")
+    for b in range(N - 1):
+        d = others[b]
+        slot = (rank - d - 1) % N
+        send(d, T.QL[:, CAP * slot:CAP * slot + CAP], T.QW[:, BL * d:BL * d + CAP], "q%d" % slot, "QW")
+
+    def order(eng, dst, src, h, r, w):
+        move(eng, dst[:, 1024 * h:1024 * h + 1024], src[:, :].indirect(T.PMU[:, 64 * h:64 * h + 64]), "PMU " + r, w)
+    order("S", T.XS, T.X, 0, "X", "XS0")
+    order("S", T.XS, T.X, 1, "X", "XS1")
+    act(T.B3[:, 0, :, 0:8], T.BLK[:, :, 0:8], AF.Copy, "BLK B3z", "B30", scale=2.0)
+    act(T.B3[:, 1, :, 8:16], T.BLK[:, :, 8:16], AF.Copy, "BLK B3z", "B31", scale=2.0)
+    for h in range(3):
+        order("S", T.TS, T.TW, h, "TW0 TW1 TW2", "TS%d" % h)
+        sums(4, 64 * h, WP, T.TS, 1024 * h, 1024 * h + 1024, True, True, "TS%d" % h)
+        if h == 0:
+            move("S", T.B3[:, 2, :, 8:16], T.BLKP[:, :, 8:16], "BLKP B3z", "B32")
+            act(wcol(WB), T.BLK[:, :, 0], AF.Copy, "BLK WSz cWB", "WS3", scale=col(cWB))
+
+    SM = T.SM
+    c0f, n16, ne, c1, e15, sd = [SM[:, 4 * j:4 * j + 4] for j in range(6)]
+    cp(c0f, T.C0[:], "C0", "c0f")
+    tt(ne, T.SF[:, 4:8], T.SF[:, 0:4], A.is_gt, "SF", "ne")
+    t1(n16, c0f, -16.0, A.mult, "c0f", "n16")
+    t1(c1, c0f, 1.0, A.add, "c0f", "c1")
+    tt(sd, T.SF[:, 0:4], T.D[:], A.subtract, "SF D", "sd")
+    tt(T.XT[:, 0:4], T.SF[:, 4:8], n16, A.add, "SF n16", "XT0")
+    tt(T.XT[:, 4:8], T.SF[:, 0:4], n16, A.add, "SF n16", "XT1")
+    tt(T.XT[:, 8:12], c1, ne, A.mult, "c1 ne", "XT2")
+    for c in range(4):
+        t1(T.P2L[:, c:36:4], T.I9[:], SM[:, c:c + 1], A.add, "I9 c0f", "P2L%d" % c)
+    tt(T.XE[:], T.XT[:, 0:12].indirect(T.U12[:, 0:12]), T.OH[:], A.mult, "XT0 XT1 XT2 U12 OH", "XE")
+    mm([(ps[3][:, 0:64], T.B3[:, 0], T.XE[:, 0:64], True, False),
+        (ps[3][:, 0:64], T.B3[:, 1], T.XE[:, 128:192], False, True)], "B30 B31 XE", "ps3")
+    mm([(ps[7][:, 0:128], T.BLK[:], T.XE[:, 0:128], True, True)], "BLK XE", "ps7")
+    P2L = "P2L0 P2L1 P2L2 P2L3"
+    t1(T.G1U[:, 4:36], T.P2L[:, 4:36], 16.0, A.mult, P2L, "G1Ua")
+    cp(T.G1U[:, 0:4], T.SF[:, 0:4], "SF", "G1Ub")
+    cp(T.P2U[:], T.P2L[:], P2L, "P2U")
+    tt(sd, sd, ne, A.mult, "sd ne", "sd")
+    t1(e15, T.SF[:, 4:8], 15.0, A.add, "SF", "e15")
+    t1(T.Z[:, 0:1024], T.XS[:, 0:1024], 0.0, A.is_equal, "XS0", "Z0")
+    ts(T.WI[:], ps[3][:, 0:64], col(cSC), col(cBA), A.mult, A.add, "ps3 cSC cBA", "WI")
+    tt(sd, sd, T.D[:], A.add, "sd D", "sd")
+    tt(e15, e15, ne, A.mult, "e15 ne", "e15")
+    t1(T.WJ[:], T.WI[:], 1, A.bitwise_and, "WI", "WJ")
+    cp(T.RU[:], sd, "sd", "RU")
+    nl = 4 if rank < N - 1 else 0
+    if nl:
+        for b in range(N):
+            cp(T.O3[:, 20 * b + 16:20 * b + 20], e15, "e15", "O3L%d" % b)
+    ts(T.PENA[:], T.WJ[:], -BIG, BIG, A.mult, A.add, "WJ", "PENA")
+
+    move("S", T.G1[:], T.TS[:, :].indirect(T.G1U[:, 0:36]), "TS0 TS1 TS2 TSz G1Ua G1Ub", "G1")
+    mm([(ps[3][:, 0:64], T.B3[:, 2], T.G1[:, 0:64], True, False)]
+       + [(ps[3][:, 0:64], slide(WP, k), T.G1[:, 64 * k + 64:64 * k + 128], False, k == 7) for k in range(8)],
+       "B32 WS0 G1", "ps3")
+
+    order("V", T.XS, T.X, 2, "X", "XS2")
+    t1(T.Z[:, 1024:2048], T.XS[:, 1024:2048], 0.0, A.is_equal, "XS1", "Z1")
+    t1(T.Z[:, 2048:M], T.XS[:, 2048:M], 0.0, A.is_equal, "XS2", "Z2")
+    cp(T.Z[:, :].indirect(T.RU[:, 0:4]), T.CT[:, 0:64], "RU CT0", "Z0 Z1 Z2")
+    H = M // 2
+
+    def fill(h):
+        scan(T.F[:, 16 + H * h:16 + H * h + H], T.Z[:, H * h:H * h + H], T.XS[:, H * h:H * h + H],
+             T.F[:, 16 + H - 1:16 + H] if h else 0.0, A.add, "Z0 Z1 Z2 XS0 XS1 XS2" + (" F0" if h else ""), "F%d" % h)
+    fill(0)
+
+    for b in range(N - 1):
+        mm([(ps[b][:, 0:CAP], T.BLKP[:], T.QL[:, CAP * b:CAP * b + CAP], True, True)], "BLKP QL%d" % b, "ps%d" % b)
+        move("S", T.QT[:, CAP * b:CAP * b + CAP], ps[b][:, 0:CAP], "ps%d" % b, "QT%d" % b)
+    R3 = 3 * CAP
+    QLr, QTr = "QL0 QL1 QL2", "QT0 QT1 QT2"
+    sums(5, 0, WI_, T.QL, 0, R3, True, True, QLr)
+    tt(T.AT[:], ps[3][:, 0:64], T.PENA[:], A.add, "ps3 PENA", "AT")
+    cp(T.O1[:, 0:48], ps[5][:, 0:48], "ps5", "O1r")
+    sums(5, 64, WI_, T.QL, 0, R3, True, False, QLr)
+    move("S", T.L2[:, 0:192], ps[4][:, 0:192], "ps4", "L2")
+    act(T.PLO[:], ps[7][:, 64:128], AF.Relu, "ps7 cNK", "PLO", bias=col(cNK), scale=BIG)
+    for n in range(9):
+        act(T.PEN[:, 64 * n:64 * n + 64], ps[7][:, 0:64], AF.Relu, "ps7 PB", "PEN%d" % n, bias=T.PB[:, n:n + 1], scale=-BIG)
+    tt(T.CMP[:, 0:R3], T.AT[:, :].indirect(T.O1[:, 0:48]), T.QT[:, 0:R3], A.is_le, "AT O1r " + QTr, "CMPr")
+    sums(5, 64, WA, T.CMP, 0, R3, False, True, "CMPr")
+    sums(6, 0, WB, T.CMP, 0, R3, True, False, "CMPr")
+    tt(T.PEN[:, 0:64], T.PEN[:, 0:64], T.PLO[:], A.subtract, "PEN0 PLO", "PEN0")
+    tt(T.P2[:], T.L2[:, :].indirect(T.P2U[:, 0:36]), T.PEN[:], A.add,
+       "L2 L2z P2U " + " ".join("PEN%d" % n for n in range(9)), "P2")
+    cp(T.O2[:, 0:48], ps[5][:, 64:112], "ps5", "O2r")
+    tt(T.CMQ[:, 0:R3], T.P2[:, :].indirect(T.O2[:, 0:48]), T.QT[:, 0:R3], A.is_le, "P2 O2r " + QTr, "CMQr")
+    sums(6, 0, W1, T.CMQ, 0, R3, False, True, "CMQr")
+    fill(1)
+    own = BL * rank
+    mm([(ps[2][:, 0:CAP], T.BLKP[:], T.QW[:, own:own + CAP], True, True)], "BLKP QW", "ps2")
+    sums(4, 0, WI_, T.QW, own, own + CAP, True, True, "QW")
+    sums(0, 0, WI_, T.QW, own, own + CAP, True, False, "QW")
+    for b in range(N - 1):
+        t1(T.O3[:, 20 * b:20 * b + 16], ps[6][:, 16 * b:16 * b + 16], -1.0, A.add, "ps6", "O3%d" % b)
+    w = CAP + 16 * nl
+    for b in range(N - 1):
+        move("V" if b == 1 else "S", T.ANS[:, BL * b:BL * b + w], T.F[:, :].indirect(T.O3[:, 20 * b:20 * b + 16 + nl]),
+             "Fz F0 F1 O3%d" % b + (" O3L%d" % b if nl else ""), "ANS%d" % b)
+        send(others[b], T.AL[:, own:own + w], T.ANS[:, BL * b:BL * b + w], "ans", "ANS%d" % b)
+
+    move("S", T.QT[:, R3:R3 + CAP], ps[2][:, 0:CAP], "ps2", "QT3")
+    cp(T.O1[:, 48:64], ps[4][:, 0:16], "ps4", "O1o")
+    tt(T.CMP[:, R3:R3 + CAP], T.AT[:, :].indirect(T.O1[:, 48:64]), T.QT[:, R3:R3 + CAP], A.is_le, "AT O1o QT3", "CMPo")
+    sums(0, 0, WA, T.CMP, R3, R3 + CAP, False, True, "CMPo")
+    sums(1, 0, WB, T.CMP, R3, R3 + CAP, True, False, "CMPo")
+    cp(T.O2[:, 48:64], ps[0][:, 0:16], "ps0", "O2o")
+    tt(T.CMQ[:, R3:R3 + CAP], T.P2[:, :].indirect(T.O2[:, 48:64]), T.QT[:, R3:R3 + CAP], A.is_le, "P2 O2o QT3", "CMQo")
+    sums(1, 0, W1, T.CMQ, R3, R3 + CAP, False, True, "CMQo")
+    t1(T.O3[:, 60:76], ps[1][:, 0:16], -1.0, A.add, "ps1", "O33")
+    cp(T.AL[:, own:own + w], T.F[:, :].indirect(T.O3[:, 60:76 + nl]), "Fz F0 F1 O33" + (" O3L3" if nl else ""), "ALo")
+
+    AL = "ALr ALo"
+    last = lambda s: T.AL[:, BL * s + CAP:BL * s + BL]
+    HQ = Q // 2
+    cs = [slice(HQ * h, HQ * h + HQ) for h in range(2)]
+    for h in range(2):
+        move("S", T.AG[:, cs[h]], T.AL[:, 0:3 * BL + CAP].indirect(T.POS[:, 24 * h:24 * h + 24]), AL + " " + POS, "AG%d" % h)
+    t1(T.CZ[:, 0:64], last(1), 0.0, A.is_equal, AL, "CZ1")
+    t1(T.CZ[:, 64:128], last(2), 0.0, A.is_equal, AL, "CZ2")
+    tt(T.CY[:], T.CZ[:, 0:64], last(0), A.mult, "CZ1 " + AL, "CY")
+    cp(T.CT[:, 64:128], last(0), AL, "CT1")
+    tt(T.CT[:, 128:192], T.CY[:], last(1), A.add, "CY " + AL, "CT2")
+    tt(T.CY[:], T.CZ[:, 64:128], T.CT[:, 128:192], A.mult, "CZ2 CT2", "CY")
+    tt(T.CT[:, 192:256], T.CY[:], last(2), A.add, "CY " + AL, "CT3")
+    for h in range(2):
+        t1(T.MZ[:, cs[h]], T.AG[:, cs[h]], 0.0, A.is_equal, "AG%d" % h, "MZ%d" % h)
+    for h in range(2):
+        tt(T.TT[:, cs[h]], T.CT[:, :].indirect(T.POS[:, 48 + 24 * h:72 + 24 * h]), T.MZ[:, cs[h]], A.mult,
+           "CT0 CT1 CT2 CT3 MZ%d " % h + POS, "TT%d" % h)
+        tt(T.YB[:, cs[h]], T.AG[:, cs[h]], T.TT[:, cs[h]], A.add, "AG%d TT%d" % (h, h), "YB%d" % h)
+        dma("Y" if h == 0 else "S", T.y[:, cs[h]], T.YB[:, cs[h]], "YB%d" % h, "y%d" % h)
+
+    count = {"V": 0, "S": 0, "P": 0, "G": 0}
+    for o in ops:
+        if o["dma"] is None and o["used"]:
+            count[o["eng"]] += 1
+            o["n"] = count[o["eng"]]
+    waited = {}
+    for o in ops:
+        need = {}
+        for d in o["deps"]:
+            sem, val = d["ext"] if d["ext"] else ((d["dma"], 16) if d["dma"] else (d["eng"], d["n"]))
+            need[sem] = max(need.get(sem, 0), val)
+        for sem, val in need.items():
+            if waited.get((o["eng"], sem), 0) < val:
+                queue[o["eng"]].wait_ge(T.sem[sem], val)
+                waited[(o["eng"], sem)] = val
+        ins = o["fn"]()
+        if o["dma"]:
+            ins.then_inc(T.sem[o["dma"]], 16)
+        elif o["used"]:
+            ins.then_inc(T.sem[o["eng"]], 1)
+    seen = {}
+    for (eng, sem), val in waited.items():
+        seen[sem] = max(seen.get(sem, 0), val)
+    g.wait_ge(T.sem.sent, nsent[0])
+    for o in ops:
+        if o["dma"] and seen.get(o["dma"], 0) < 16:
+            queue[o["eng"]].wait_ge(T.sem[o["dma"]], 16)

@@ -1,25 +1,25 @@
+from concourse.bass import DstId, RemoteDMATransfer
 from concourse.mybir import AluOpType as A, AxisListType, ActivationFunctionType as AF
 
 M, NI, Q, CAP = 3072, 64, 768, 256
-BL = CAP + NI
 BIG = float(2 ** 23)
 F32, BF, I32, U16 = "float32", "bfloat16", "int32", "uint16"
 _S = {
-    BF: dict(X=M, XS=M, Z=M + 512, F=M + 16, TW=M, TS=M + 144, TP=576, QP=192, QR=Q, QW=4 * BL, QL=3 * CAP, E=192,
+    BF: dict(X=M, XS=M, Z=M + 512, F=M + 16, TW=M, TS=M + 144, TP=576, QP=192, QR=Q, QW=4 * CAP, QL=3 * CAP, E=192,
              RST=192, ONE=128, CR=192, C16=128, CM16=128, TMPA=128, TMPB=128, TMPC=128, CW=32, BLK=[8, 16], TRI=128,
-             BLKP=[8, 16], B3=[3, 8, 16], WS=720, OH=192, XE=192, G1=576, CMP=4 * CAP, CMQ=4 * CAP, ANS=3 * BL,
-             AL=4 * BL, CT=256, CZ=128, CY=64, AG=Q, MZ=Q, TT=Q, YB=Q),
+             BLKP=[8, 16], B3=[3, 8, 16], WS=720, OH=192, XE=192, G1=576, CMP=4 * CAP, CMQ=4 * CAP, ANS=3 * CAP,
+             AL=4 * CAP, CT=384, CZ=128, CY=64, AG=Q, MZ=Q, CG=Q, YB=Q),
     F32: dict(QF=48, QF2=48, QT=4 * CAP, CN=192, CN2=192, CN3=96, PC=[6, 16], TI=[6, 2, 16], TO=[6, 2, 16], R=[6, 16],
               KC=24, IO=192, GR=16, TWO=8, GT=16, I9=9, PB=9, D=4, SF=8, SM=32, XT=16, P2L=36, PENA=64, PEN=576,
               PLO=64, L2=208, AT=64, P2=576),
     I32: dict(PM=192, TB=192, TI3=576, QB=96, QI3=144, QS=48, QH=48, IP=4, I12=12, SE=8, C0=4, WI=64, WJ=64),
-    U16: dict(PMU=192, POS=96, U12=12, P2U=36, G1U=36, RU=4, O1=64, O2=64, O3=80),
+    U16: dict(PMU=192, POS=96, U12=12, P2U=36, G1U=36, RU=4, LU=4, O1=64, O2=64, O3=64),
 }
 SCRATCH = {_n: ("sbuf", [128] + (_c if isinstance(_c, list) else [_c]), _d) for _d in _S for _n, _c in _S[_d].items()}
 for _b in range(8):
     SCRATCH["ps%d" % _b] = ("psum", [128, 512], F32)
 
-SEMAPHORES = ["V", "S", "P", "G", "sent", "q0", "q1", "q2", "ans"] + ["d%d" % _i for _i in range(24)]
+SEMAPHORES = ["V", "S", "P", "G", "sent", "q0", "q1", "q2", "ans", "last"] + ["d%d" % _i for _i in range(24)]
 
 
 def rank_program(g, core, T, topo):
@@ -82,6 +82,9 @@ def rank_program(g, core, T, topo):
     def act(out, in_, f, r, w, **kw):
         op("S", lambda: S.activation(out, in_, f, **kw), r, w)
 
+    def lin(out, in_, scale, bias, r, w):
+        act(out, in_, AF.Identity, r, w, scale=scale, bias=bias)
+
     def move(eng, out, in_, r, w):
         if eng == "S":
             act(out, in_, AF.Copy, r, w)
@@ -115,10 +118,14 @@ def rank_program(g, core, T, topo):
         nsent[0] += len(topo.engines(core, dst))
         op("G", lambda: g.remote_dma(out, in_, T.sem[sem], T.sem.sent, pid, rid, mask), r, "")
 
+    def shared(src):
+        sets = [topo.engines(T.cores[src], T.cores[o]) for o in range(N) if o != src]
+        return [e for e in sets[0] if all(e in s for s in sets)]
+
     ps = [T["ps%d" % b] for b in range(8)]
     KC = T.KC
     col = lambda j: KC[:, j:j + 1]
-    cK, cD1, cD0, cWB, cPW, cSC, cS0, cBA, cNK, cM7, cT1, cT2 = range(12)
+    cK, cD1, cD0, cWB, cPW, cSC, cS0, cBA, cNK, cM7, cT1, cT2, cK1 = range(13)
 
     def slide(x, m):
         return T.WS[:, 144 * x + 15 - m:144 * x + 143 - m]
@@ -134,14 +141,15 @@ def rank_program(g, core, T, topo):
     for b in range(N - 1):
         landing("QL%d" % b, "q%d" % b, len(topo.engines(T.cores[others[b]], core)))
     landing("ALr", "ans", sum(len(topo.engines(T.cores[o], core)) for o in others))
+    landing("Lr", "last", sum(len(shared(o)) for o in others if o < N - 1))
 
     dma("Y", T.QB[:, 0:48], T.qt[:], "", "QBt")
     dma("S", T.QB[:, 48:96], T.qi[:], "", "QBi")
     dma("Y", T.TB[:], T.times[:], "", "TB")
     dma("S", T.PM[:], T.pm[:], "", "PM")
-    dma("Y", T.X[:], T.x[:], "", "X")
     dma("S", T.SE[:, 0:4], T.starts[:, 0:64], "", "SEs")
     dma("S", T.SE[:, 4:8], T.starts[:, 1:65], "", "SEe")
+    dma("Y", T.X[:], T.x[:], "", "X")
 
     ms(T.C16[:], 1.0 / 16, "C16")
     ms(T.CM16[:], -1.0 / 16, "CM16")
@@ -149,25 +157,25 @@ def rank_program(g, core, T, topo):
     ms(T.ONE[:], 1.0, "ONE")
     iota(T.IP[:, 0:1], [[0, 1]], 0, 1, "IP0", False)
     iota(T.IO[:], [[0, 12], [1, 16]], 0, 0, "IO")
-    iota(T.I9[:], [[1, 9]], 0, 0, "I9")
     grp, neg = [[-16, 8], [0, 16]], [[16, 8], [0, 16]]
     sel(T.TMPA[:], T.C16[:], grp, A.is_ge, 0, 1, "C16", "TMPA")
     sel(T.TMPB[:], T.CM16[:], [[-16, 8], [-1, 16]], A.is_gt, 0, 1, "CM16", "TMPB")
     sel(T.BLK[:], T.TMPA[:], neg, A.is_ge, 15, -1, "TMPA", "BLK")
     sel(T.TRI[:], T.TMPB[:], neg, A.is_ge, 15, -1, "TMPB", "TRI")
-    iota(T.CR[0:1, :], [[BL // 16, 4], [0, 48]], 0, 0, "CR")
+    iota(T.CR[0:1, :], [[CAP // 16, 4], [0, 48]], 0, 0, "CR")
+    iota(T.I9[:], [[1, 9]], 0, 0, "I9")
     iota(T.I12[:], [[1, 12]], 0, 0, "I12", False)
     iota(T.D[:], [[1, 4]], M, 4, "D")
     iota(T.WS[:], [[0, 720]], 0, 0, "WSz")
     iota(T.CW[:, 0:16], [[48, 2], [0, 8]], 16, 0, "CW")
     sel(T.TMPC[:], T.ONE[:], grp, A.is_ge, 0, 1, "ONE", "TMPC")
     sel(T.CW[:, 16:24], T.CW[:, 8:16], [[-16, 8]], A.is_ge, 0, 1, "CW", "CWb")
-    sel(T.BLKP[:], T.TMPC[:], neg, A.is_ge, 2, -1, "TMPC", "BLKP")
     sel(wcol(WP), T.TMPC[:, 0:128:16], [[16, 8]], A.is_ge, 2, -1, "TMPC WSz", "WS0")
+    iota(T.B3[:], [[0, 384]], 0, 0, "B3z")
+    sel(T.BLKP[:], T.TMPC[:], neg, A.is_ge, 2, -1, "TMPC", "BLKP")
     sel(wcol(WI_), T.CW[:, 0:8], [[-16, 8]], A.is_equal, -3, 1, "CW WSz", "WS1")
     sel(wcol(WA), T.CW[:, 16:24], [[16, 8]], A.is_ge, 7, -1, "CWb WSz", "WS2")
     sel(wcol(W1), T.TMPC[:, 0:128:16], [[16, 8]], A.is_ge, 15, -1, "TMPC WSz", "WS4")
-    iota(T.B3[:], [[0, 384]], 0, 0, "B3z")
     iota(T.TS[:, M:M + 144], [[0, 144]], 0, 0, "TSz")
     iota(T.CT[:, 0:64], [[0, 64]], 0, 0, "CT0")
     iota(T.F[:, 0:16], [[0, 16]], 0, 0, "Fz")
@@ -184,17 +192,14 @@ def rank_program(g, core, T, topo):
     cp(KC[:, 0:2], T.IP[:, 1:3], "IP1 IP2", "cK")
     scan(T.GR[:, 8:16], T.TWO[:], T.TWO[:], 1.0, A.max, "TWO", "GRb")
     ts(T.OH[:], T.IO[:], col(cK), 16.0, A.is_equal, A.mult, "IO cK", "OH")
-    ts(col(cD0), col(cD1), -1.0, 1.0, A.mult, A.add, "cK", "cD0")
     t1(col(cM7), col(cK), 7.0, A.is_le, "cK", "cM7")
-    ts(col(cT1), col(cK), -1.0 / 16, 239.0 / 256, A.mult, A.add, "cK", "cT1")
-    tt(T.GT[:], T.GR[:], T.OH[:, 0:16], A.mult, "GRa GRb OH", "GT")
-    ts(T.PB[:], T.I9[:], 16.0, col(cK), A.mult, A.add, "I9 cK", "PB")
-    t1(col(cNK), col(cK), -BIG, A.mult, "cK", "cNK")
-    op("V", lambda: V.tensor_reduce(col(cPW), T.GT[:], AxisListType.X, A.add), "GT", "cPW")
-    ts(col(cBA), col(cT1), col(cM7), -0.5 + 1.0 / 512, A.mult, A.add, "cT1 cM7", "cBA")
-    t1(col(cT2), col(cM7), -65280.0, A.mult, "cM7", "cT2")
-    op("V", lambda: V.reciprocal(col(cS0), col(cPW)), "cPW", "cS0")
-    ts(T.PB[:], T.PB[:], 1.0, BIG, A.add, A.mult, "PB", "PB")
+    lin(col(cD0), col(cD1), -1.0, 1.0, "cK", "cD0")
+    lin(col(cT1), col(cK), -1.0 / 16, 239.0 / 256, "cK", "cT1")
+    lin(col(cK1), col(cK), BIG, BIG, "cK", "cK1")
+    lin(col(cNK), col(cK), -BIG, 0.0, "cK", "cNK")
+    lin(col(cT2), col(cM7), -65280.0, 0.0, "cM7", "cT2")
+    lin(col(cBA), col(cT1), col(cM7), -0.5 + 1.0 / 512, "cT1 cM7", "cBA")
+    lin(T.PB[:], T.I9[:], 16.0 * BIG, col(cK1), "I9 cK1", "PB")
 
     masks = (0x3F8000, 0x7F80, 0x7F)
     for j in range(3):
@@ -221,50 +226,52 @@ def rank_program(g, core, T, topo):
     for j in range(3):
         dma("Y", T.TW[j:128:16, :], T.TP[:, 192 * j:192 * j + 192], "TP TWz0 TWz1 TWz2", "TW%d" % j)
     tt(T.CN2[:], T.CN[:], ps[1][:, 0:192], A.add, "CN ps1", "CN2")
-    ts(T.QF2[:], T.QS[:], 4.0, 1.0 / 16, A.mult, A.add, "QS", "QF2")
-    tt(T.CN[:], T.CN2[:], T.E[:], A.mult, "CN2 " + Es, "CN")
-    tt(T.PC[:, 3:6, :], T.QF2[:], T.QP[:, 144:192], A.add, "QF2 QP3", "PC1")
-    tt(T.CN3[:], T.CN[:, 0:96], T.CN[:, 96:192], A.add, "CN", "CN3")
     cp(T.PMU[:], T.PM[:], "PM", "PMU")
+    tt(T.CN[:], T.CN2[:], T.E[:], A.mult, "CN2 " + Es, "CN")
+    ts(T.QF2[:], T.QS[:], 4.0, 1.0 / 16, A.mult, A.add, "QS", "QF2")
+    tt(T.CN3[:], T.CN[:, 0:96], T.CN[:, 96:192], A.add, "CN", "CN3")
+    tt(T.PC[:, 3:6, :], T.QF2[:], T.QP[:, 144:192], A.add, "QF2 QP3", "PC1")
     tt(T.PC[:, 0:3, :], T.CN3[:, 0:48], T.CN3[:, 48:96], A.add, "CN3", "PC0")
-    ts(col(cWB), col(cPW), 8.0, col(cT2), A.mult, A.add, "cPW cT2", "cWB")
     t1(T.TI[:, :, 0, :], T.PC[:], col(cD0), A.mult, "PC0 PC1 cD0", "TIa")
     t1(T.TI[:, :, 1, :], T.PC[:], col(cD1), A.mult, "PC0 PC1 cK", "TIb")
-    t1(col(cSC), col(cS0), 16.0, A.mult, "cS0", "cSC")
     op("V", lambda: V.transpose(T.TO[:], T.TI[:]), "TIa TIb", "TO")
-    cp(T.U12[:], T.I12[:], "I12", "U12")
     tt(T.R[:], T.TO[:, :, 0, :], T.TO[:, :, 1, :], A.add, "TO", "R")
-    cp(T.SF[:], T.SE[:], "SEs SEe", "SF")
     for u in range(3):
         ts(T.POS[:, u:96:3], T.R[:, u:6:3, :], 16.0, -1.0, A.mult, A.add, "R", "POS%d" % u)
     POS = "POS0 POS1 POS2"
-    t1(T.C0[:], T.SE[:, 0:4], 4, A.arith_shift_right, "SEs", "C0")
     cp(T.QW[:, :].indirect(T.POS[:, 0:48]), T.QR[:], POS + " QR0 QR1 QR2 QR3", "QW")
     for b in range(N - 1):
         d = others[b]
         slot = (rank - d - 1) % N
-        send(d, T.QL[:, CAP * slot:CAP * slot + CAP], T.QW[:, BL * d:BL * d + CAP], "q%d" % slot, "QW")
+        send(d, T.QL[:, CAP * slot:CAP * slot + CAP], T.QW[:, CAP * d:CAP * d + CAP], "q%d" % slot, "QW")
 
-    def order(eng, dst, src, h, r, w):
-        move(eng, dst[:, 1024 * h:1024 * h + 1024], src[:, :].indirect(T.PMU[:, 64 * h:64 * h + 64]), "PMU " + r, w)
-    order("S", T.XS, T.X, 0, "X", "XS0")
-    order("S", T.XS, T.X, 1, "X", "XS1")
+    def order(eng, dst, src, a, b, r, w):
+        move(eng, dst[:, a:b], src[:, :].indirect(T.PMU[:, a // 16:b // 16]), "PMU " + r, w)
+
+    def times(h):
+        order("S", T.TS, T.TW, 1024 * h, 1024 * h + 1024, "TW0 TW1 TW2", "TS%d" % h)
+        sums(4, 64 * h, WP, T.TS, 1024 * h, 1024 * h + 1024, True, True, "TS%d" % h)
+    order("S", T.XS, T.X, 0, 1024, "X", "XS0")
+    order("S", T.XS, T.X, 1024, 2048, "X", "XS1")
+    times(0)
     act(T.B3[:, 0, :, 0:8], T.BLK[:, :, 0:8], AF.Copy, "BLK B3z", "B30", scale=2.0)
     act(T.B3[:, 1, :, 8:16], T.BLK[:, :, 8:16], AF.Copy, "BLK B3z", "B31", scale=2.0)
-    for h in range(3):
-        order("S", T.TS, T.TW, h, "TW0 TW1 TW2", "TS%d" % h)
-        sums(4, 64 * h, WP, T.TS, 1024 * h, 1024 * h + 1024, True, True, "TS%d" % h)
-        if h == 0:
-            move("S", T.B3[:, 2, :, 8:16], T.BLKP[:, :, 8:16], "BLKP B3z", "B32")
-            act(wcol(WB), T.BLK[:, :, 0], AF.Copy, "BLK WSz cWB", "WS3", scale=col(cWB))
+    order("S", T.XS, T.X, 2048, 2560, "X", "XS2")
+    own, R3 = CAP * rank, 3 * CAP
+    mm([(ps[2][:, 0:CAP], T.BLKP[:], T.QW[:, own:own + CAP], True, True)], "BLKP QW", "ps2")
+    sums(6, 0, WI_, T.QW, own, own + CAP, True, True, "QW")
 
     SM = T.SM
     c0f, n16, ne, c1, e15, sd = [SM[:, 4 * j:4 * j + 4] for j in range(6)]
+    t1(T.C0[:], T.SE[:, 0:4], 4, A.arith_shift_right, "SEs", "C0")
+    cp(T.SF[:], T.SE[:], "SEs SEe", "SF")
+    cp(T.U12[:], T.I12[:], "I12", "U12")
     cp(c0f, T.C0[:], "C0", "c0f")
     tt(ne, T.SF[:, 4:8], T.SF[:, 0:4], A.is_gt, "SF", "ne")
+    tt(T.GT[:], T.GR[:], T.OH[:, 0:16], A.mult, "GRa GRb OH", "GT")
     t1(n16, c0f, -16.0, A.mult, "c0f", "n16")
     t1(c1, c0f, 1.0, A.add, "c0f", "c1")
-    tt(sd, T.SF[:, 0:4], T.D[:], A.subtract, "SF D", "sd")
+    op("V", lambda: V.tensor_reduce(col(cPW), T.GT[:], AxisListType.X, A.add), "GT", "cPW")
     tt(T.XT[:, 0:4], T.SF[:, 4:8], n16, A.add, "SF n16", "XT0")
     tt(T.XT[:, 4:8], T.SF[:, 0:4], n16, A.add, "SF n16", "XT1")
     tt(T.XT[:, 8:12], c1, ne, A.mult, "c1 ne", "XT2")
@@ -274,53 +281,62 @@ def rank_program(g, core, T, topo):
     mm([(ps[3][:, 0:64], T.B3[:, 0], T.XE[:, 0:64], True, False),
         (ps[3][:, 0:64], T.B3[:, 1], T.XE[:, 128:192], False, True)], "B30 B31 XE", "ps3")
     mm([(ps[7][:, 0:128], T.BLK[:], T.XE[:, 0:128], True, True)], "BLK XE", "ps7")
+    times(1)
+    times(2)
     P2L = "P2L0 P2L1 P2L2 P2L3"
+    op("V", lambda: V.reciprocal(col(cS0), col(cPW)), "cPW", "cS0")
     t1(T.G1U[:, 4:36], T.P2L[:, 4:36], 16.0, A.mult, P2L, "G1Ua")
     cp(T.G1U[:, 0:4], T.SF[:, 0:4], "SF", "G1Ub")
+    tt(sd, T.SF[:, 0:4], T.D[:], A.subtract, "SF D", "sd")
     cp(T.P2U[:], T.P2L[:], P2L, "P2U")
+    t1(col(cSC), col(cS0), 16.0, A.mult, "cS0", "cSC")
     tt(sd, sd, ne, A.mult, "sd ne", "sd")
     t1(e15, T.SF[:, 4:8], 15.0, A.add, "SF", "e15")
-    t1(T.Z[:, 0:1024], T.XS[:, 0:1024], 0.0, A.is_equal, "XS0", "Z0")
-    ts(T.WI[:], ps[3][:, 0:64], col(cSC), col(cBA), A.mult, A.add, "ps3 cSC cBA", "WI")
+    t1(T.Z[:, 0:2048], T.XS[:, 0:2048], 0.0, A.is_equal, "XS0 XS1", "Z0")
     tt(sd, sd, T.D[:], A.add, "sd D", "sd")
     tt(e15, e15, ne, A.mult, "e15 ne", "e15")
-    t1(T.WJ[:], T.WI[:], 1, A.bitwise_and, "WI", "WJ")
+    order("V", T.XS, T.X, 2560, M, "X", "XS3")
     cp(T.RU[:], sd, "sd", "RU")
-    nl = 4 if rank < N - 1 else 0
-    if nl:
-        for b in range(N):
-            cp(T.O3[:, 20 * b + 16:20 * b + 20], e15, "e15", "O3L%d" % b)
+    ts(T.WI[:], ps[3][:, 0:64], col(cSC), col(cBA), A.mult, A.add, "ps3 cSC cBA", "WI")
+    t1(T.Z[:, 2048:M], T.XS[:, 2048:M], 0.0, A.is_equal, "XS2 XS3", "Z1")
+    t1(T.WJ[:], T.WI[:], 1, A.bitwise_and, "WI", "WJ")
+    cp(T.O1[:, 48:64], ps[6][:, 0:16], "ps6", "O1o")
+    cp(T.Z[:, :].indirect(T.RU[:, 0:4]), T.CT[:, 0:64], "RU CT0", "Z0 Z1")
     ts(T.PENA[:], T.WJ[:], -BIG, BIG, A.mult, A.add, "WJ", "PENA")
+    cp(T.LU[:], e15, "e15", "LU")
 
+    move("S", T.B3[:, 2, :, 8:16], T.BLKP[:, :, 8:16], "BLKP B3z", "B32")
     move("S", T.G1[:], T.TS[:, :].indirect(T.G1U[:, 0:36]), "TS0 TS1 TS2 TSz G1Ua G1Ub", "G1")
     mm([(ps[3][:, 0:64], T.B3[:, 2], T.G1[:, 0:64], True, False)]
        + [(ps[3][:, 0:64], slide(WP, k), T.G1[:, 64 * k + 64:64 * k + 128], False, k == 7) for k in range(8)],
        "B32 WS0 G1", "ps3")
+    move("S", T.QT[:, R3:R3 + CAP], ps[2][:, 0:CAP], "ps2", "QT3")
+    lin(col(cWB), col(cPW), 8.0, col(cT2), "cPW cT2", "cWB")
+    move("S", T.L2[:, 0:192], ps[4][:, 0:192], "ps4", "L2")
+    act(wcol(WB), T.BLK[:, :, 0], AF.Copy, "BLK WSz cWB", "WS3", scale=col(cWB))
 
-    order("V", T.XS, T.X, 2, "X", "XS2")
-    t1(T.Z[:, 1024:2048], T.XS[:, 1024:2048], 0.0, A.is_equal, "XS1", "Z1")
-    t1(T.Z[:, 2048:M], T.XS[:, 2048:M], 0.0, A.is_equal, "XS2", "Z2")
-    cp(T.Z[:, :].indirect(T.RU[:, 0:4]), T.CT[:, 0:64], "RU CT0", "Z0 Z1 Z2")
-    H = M // 2
-
-    def fill(h):
-        scan(T.F[:, 16 + H * h:16 + H * h + H], T.Z[:, H * h:H * h + H], T.XS[:, H * h:H * h + H],
-             T.F[:, 16 + H - 1:16 + H] if h else 0.0, A.add, "Z0 Z1 Z2 XS0 XS1 XS2" + (" F0" if h else ""), "F%d" % h)
-    fill(0)
+    scan(T.F[:, 16:16 + M], T.Z[:, 0:M], T.XS[:], 0.0, A.add, "Z0 Z1 XS0 XS1 XS2 XS3", "F")
+    lcol = (64, 256, 320)
 
     for b in range(N - 1):
         mm([(ps[b][:, 0:CAP], T.BLKP[:], T.QL[:, CAP * b:CAP * b + CAP], True, True)], "BLKP QL%d" % b, "ps%d" % b)
         move("S", T.QT[:, CAP * b:CAP * b + CAP], ps[b][:, 0:CAP], "ps%d" % b, "QT%d" % b)
-    R3 = 3 * CAP
     QLr, QTr = "QL0 QL1 QL2", "QT0 QT1 QT2"
     sums(5, 0, WI_, T.QL, 0, R3, True, True, QLr)
     tt(T.AT[:], ps[3][:, 0:64], T.PENA[:], A.add, "ps3 PENA", "AT")
     cp(T.O1[:, 0:48], ps[5][:, 0:48], "ps5", "O1r")
     sums(5, 64, WI_, T.QL, 0, R3, True, False, QLr)
-    move("S", T.L2[:, 0:192], ps[4][:, 0:192], "ps4", "L2")
     act(T.PLO[:], ps[7][:, 64:128], AF.Relu, "ps7 cNK", "PLO", bias=col(cNK), scale=BIG)
     for n in range(9):
         act(T.PEN[:, 64 * n:64 * n + 64], ps[7][:, 0:64], AF.Relu, "ps7 PB", "PEN%d" % n, bias=T.PB[:, n:n + 1], scale=-BIG)
+    if rank < N - 1:
+        mine = T.CT[:, lcol[rank]:lcol[rank] + NI]
+        move("S", mine, T.F[:, :].indirect(T.LU[:, 0:4]), "Fz F LU", "Lo")
+        ids = [topo.addr(T.cores[o], core) for o in others]
+        nsent[0] += len(shared(rank))
+        op("G", lambda: g.remote_dma_fused(
+            [RemoteDMATransfer(dst_ids=[DstId(rid=a[0], pnc=a[1]) for a in ids], dma_engine_mask=sum(1 << e for e in shared(rank)),
+                               remote_sem=T.sem["last"], srcs=[mine], dsts=[mine for a in ids])], local_sem=T.sem.sent), "Lo", "")
     tt(T.CMP[:, 0:R3], T.AT[:, :].indirect(T.O1[:, 0:48]), T.QT[:, 0:R3], A.is_le, "AT O1r " + QTr, "CMPr")
     sums(5, 64, WA, T.CMP, 0, R3, False, True, "CMPr")
     sums(6, 0, WB, T.CMP, 0, R3, True, False, "CMPr")
@@ -330,50 +346,42 @@ def rank_program(g, core, T, topo):
     cp(T.O2[:, 0:48], ps[5][:, 64:112], "ps5", "O2r")
     tt(T.CMQ[:, 0:R3], T.P2[:, :].indirect(T.O2[:, 0:48]), T.QT[:, 0:R3], A.is_le, "P2 O2r " + QTr, "CMQr")
     sums(6, 0, W1, T.CMQ, 0, R3, False, True, "CMQr")
-    fill(1)
-    own = BL * rank
-    mm([(ps[2][:, 0:CAP], T.BLKP[:], T.QW[:, own:own + CAP], True, True)], "BLKP QW", "ps2")
-    sums(4, 0, WI_, T.QW, own, own + CAP, True, True, "QW")
-    sums(0, 0, WI_, T.QW, own, own + CAP, True, False, "QW")
-    for b in range(N - 1):
-        t1(T.O3[:, 20 * b:20 * b + 16], ps[6][:, 16 * b:16 * b + 16], -1.0, A.add, "ps6", "O3%d" % b)
-    w = CAP + 16 * nl
-    for b in range(N - 1):
-        move("V" if b == 1 else "S", T.ANS[:, BL * b:BL * b + w], T.F[:, :].indirect(T.O3[:, 20 * b:20 * b + 16 + nl]),
-             "Fz F0 F1 O3%d" % b + (" O3L%d" % b if nl else ""), "ANS%d" % b)
-        send(others[b], T.AL[:, own:own + w], T.ANS[:, BL * b:BL * b + w], "ans", "ANS%d" % b)
-
-    move("S", T.QT[:, R3:R3 + CAP], ps[2][:, 0:CAP], "ps2", "QT3")
-    cp(T.O1[:, 48:64], ps[4][:, 0:16], "ps4", "O1o")
     tt(T.CMP[:, R3:R3 + CAP], T.AT[:, :].indirect(T.O1[:, 48:64]), T.QT[:, R3:R3 + CAP], A.is_le, "AT O1o QT3", "CMPo")
-    sums(0, 0, WA, T.CMP, R3, R3 + CAP, False, True, "CMPo")
-    sums(1, 0, WB, T.CMP, R3, R3 + CAP, True, False, "CMPo")
-    cp(T.O2[:, 48:64], ps[0][:, 0:16], "ps0", "O2o")
-    tt(T.CMQ[:, R3:R3 + CAP], T.P2[:, :].indirect(T.O2[:, 48:64]), T.QT[:, R3:R3 + CAP], A.is_le, "P2 O2o QT3", "CMQo")
-    sums(1, 0, W1, T.CMQ, R3, R3 + CAP, False, True, "CMQo")
-    t1(T.O3[:, 60:76], ps[1][:, 0:16], -1.0, A.add, "ps1", "O33")
-    cp(T.AL[:, own:own + w], T.F[:, :].indirect(T.O3[:, 60:76 + nl]), "Fz F0 F1 O33" + (" O3L3" if nl else ""), "ALo")
+    sums(4, 0, WI_, T.QW, own, own + CAP, True, False, "QW")
+    sums(4, 0, WA, T.CMP, R3, R3 + CAP, False, True, "CMPo")
+    sums(3, 0, WB, T.CMP, R3, R3 + CAP, True, False, "CMPo")
+    t1(T.O3[:, 0:48], ps[6][:, 0:48], -1.0, A.add, "ps6", "O3r")
+    for b in range(N - 1):
+        move("V" if b == 1 else "S", T.ANS[:, CAP * b:CAP * b + CAP], T.F[:, :].indirect(T.O3[:, 16 * b:16 * b + 16]),
+             "Fz F O3r", "ANS%d" % b)
+        send(others[b], T.AL[:, own:own + CAP], T.ANS[:, CAP * b:CAP * b + CAP], "ans", "ANS%d" % b)
 
-    AL = "ALr ALo"
-    last = lambda s: T.AL[:, BL * s + CAP:BL * s + BL]
-    HQ = Q // 2
-    cs = [slice(HQ * h, HQ * h + HQ) for h in range(2)]
-    for h in range(2):
-        move("S", T.AG[:, cs[h]], T.AL[:, 0:3 * BL + CAP].indirect(T.POS[:, 24 * h:24 * h + 24]), AL + " " + POS, "AG%d" % h)
-    t1(T.CZ[:, 0:64], last(1), 0.0, A.is_equal, AL, "CZ1")
-    t1(T.CZ[:, 64:128], last(2), 0.0, A.is_equal, AL, "CZ2")
-    tt(T.CY[:], T.CZ[:, 0:64], last(0), A.mult, "CZ1 " + AL, "CY")
-    cp(T.CT[:, 64:128], last(0), AL, "CT1")
-    tt(T.CT[:, 128:192], T.CY[:], last(1), A.add, "CY " + AL, "CT2")
-    tt(T.CY[:], T.CZ[:, 64:128], T.CT[:, 128:192], A.mult, "CZ2 CT2", "CY")
-    tt(T.CT[:, 192:256], T.CY[:], last(2), A.add, "CY " + AL, "CT3")
-    for h in range(2):
+    L = "Lr Lo"
+    last = lambda s: T.CT[:, lcol[s]:lcol[s] + NI]
+    t1(T.CZ[:], T.CT[:, 256:384], 0.0, A.is_equal, L, "CZ")
+    tt(T.CY[:], T.CZ[:, 0:64], last(0), A.mult, "CZ " + L, "CY")
+    tt(T.CT[:, 128:192], T.CY[:], last(1), A.add, "CY " + L, "CT2")
+    tt(T.CY[:], T.CZ[:, 64:128], T.CT[:, 128:192], A.mult, "CZ CT2", "CY")
+    tt(T.CT[:, 192:256], T.CY[:], last(2), A.add, "CY " + L, "CT3")
+    cs = [slice(CAP * h, CAP * h + CAP) for h in range(3)]
+    move("S", T.CG[:], T.CT[:, 0:256].indirect(T.POS[:, 48:96]), "CT0 CT2 CT3 " + L + " " + POS, "CG")
+    for h in range(3):
+        move("S", ps[h][:, 0:CAP], T.CG[:, cs[h]], "CG", "ps%d" % h)
+
+    cp(T.O2[:, 48:64], ps[4][:, 0:16], "ps4", "O2o")
+    tt(T.CMQ[:, R3:R3 + CAP], T.P2[:, :].indirect(T.O2[:, 48:64]), T.QT[:, R3:R3 + CAP], A.is_le, "P2 O2o QT3", "CMQo")
+    sums(3, 0, W1, T.CMQ, R3, R3 + CAP, False, True, "CMQo")
+    t1(T.O3[:, 48:64], ps[3][:, 0:16], -1.0, A.add, "ps3", "O3o")
+    cp(T.AL[:, own:own + CAP], T.F[:, :].indirect(T.O3[:, 48:64]), "Fz F O3o", "ALo")
+
+    for h in range(3):
+        move("S", T.AG[:, cs[h]], T.AL[:, :].indirect(T.POS[:, 16 * h:16 * h + 16]), "ALr ALo " + POS, "AG%d" % h)
+    for h in range(3):
+        bank = "ps%d" % h
         t1(T.MZ[:, cs[h]], T.AG[:, cs[h]], 0.0, A.is_equal, "AG%d" % h, "MZ%d" % h)
-    for h in range(2):
-        tt(T.TT[:, cs[h]], T.CT[:, :].indirect(T.POS[:, 48 + 24 * h:72 + 24 * h]), T.MZ[:, cs[h]], A.mult,
-           "CT0 CT1 CT2 CT3 MZ%d " % h + POS, "TT%d" % h)
-        tt(T.YB[:, cs[h]], T.AG[:, cs[h]], T.TT[:, cs[h]], A.add, "AG%d TT%d" % (h, h), "YB%d" % h)
-        dma("Y" if h == 0 else "S", T.y[:, cs[h]], T.YB[:, cs[h]], "YB%d" % h, "y%d" % h)
+        tt(ps[h][:, 0:CAP], T.MZ[:, cs[h]], ps[h][:, 0:CAP], A.mult, "MZ%d %s" % (h, bank), bank)
+        tt(T.YB[:, cs[h]], T.AG[:, cs[h]], ps[h][:, 0:CAP], A.add, "AG%d %s" % (h, bank), "YB%d" % h)
+        dma("S" if h == 2 else "Y", T.y[:, cs[h]], T.YB[:, cs[h]], "YB%d" % h, "y%d" % h)
 
     count = {"V": 0, "S": 0, "P": 0, "G": 0}
     for o in ops:

@@ -3,23 +3,48 @@ from concourse.mybir import AluOpType as A, AxisListType, ActivationFunctionType
 
 M, NI, Q, CAP = 3072, 64, 768, 256
 BIG = float(2 ** 23)
+RND = 1.5 * 2.0 ** 43
+CB = M + 96
+FB = CB + 16 * NI + 1
+DUMP = M + 16
+R7, R14 = 1.5 * 2.0 ** 30, 1.5 * 2.0 ** 37
+EARLY = ("ONE TWz0 IP0 TMPA IO TRI I4 BLK TRC I12 TWO GRa L2z TWz2 FL0 FL1 FL2 FL3 QRz IP1 cK D QW DK TWz1 BIGT WSz IDN WS0 "
+         "BLKP TSz Zz").split()
+HELP1 = (2,)
+HELP2 = (2,)
+XCUT = (0, 1280, 2048, M)
+XENG = "SSV"
+TCUT = (0, 1024, 2048, M)
+TENG = "SSS"
+STEPS = ("load tpieces qpieces slot pmu power scales bounds scatter cols x0 lists t0 x2 z0 x1 z1 z2 fill s3 f0 u0 bits t1 t2 "
+         "f1 u1 s0 f2 at qa o1 weights s1 s2 head ib qb u2 l1 o2 carry p2 wba l2a refill spread o3a wbo ansa l2o o3o end").split()
+LAST = 11000
+GATHER, SCATTER = 1.56, 3.8
+CYC = 0.85
+WAKE = 100
+LOCAL = 1000
+REMOTE = 2200
+ROUNDS = 0
+GROUPS = ((7, (0, 1, 2), "a"),)
+AENG = "VSS"
+LONG = 400
+GUARD = 0
 F32, BF, I32, U16 = "float32", "bfloat16", "int32", "uint16"
 _S = {
-    BF: dict(X=M, XS=M, Z=M + 512, F=M + 16, TW=M, TS=M + 144, TP=576, QP=192, QR=Q, QW=4 * CAP, QL=3 * CAP, E=192,
-             RST=192, ONE=128, CR=192, C16=128, CM16=128, TMPA=128, TMPB=128, TMPC=128, CW=32, BLK=[8, 16], TRI=128,
-             BLKP=[8, 16], B3=[3, 8, 16], WS=720, OH=192, XE=192, G1=576, CMP=4 * CAP, CMQ=4 * CAP, ANS=3 * CAP,
-             AL=4 * CAP, CT=384, CZ=128, CY=64, AG=Q, MZ=Q, CG=Q, YB=Q),
-    F32: dict(QF=48, QF2=48, QT=4 * CAP, CN=192, CN2=192, CN3=96, PC=[6, 16], TI=[6, 2, 16], TO=[6, 2, 16], R=[6, 16],
-              KC=24, IO=192, GR=16, TWO=8, GT=16, I9=9, PB=9, D=4, SF=8, SM=32, XT=16, P2L=36, PENA=64, PEN=576,
-              PLO=64, L2=208, AT=64, P2=576),
-    I32: dict(PM=192, TB=192, TI3=576, QB=96, QI3=144, QS=48, QH=48, IP=4, I12=12, SE=8, C0=4, WI=64, WJ=64),
-    U16: dict(PMU=192, POS=96, U12=12, P2U=36, G1U=36, RU=4, LU=4, O1=64, O2=64, O3=64),
+    BF: dict(X=M, BUF=CB + 1024 + CB, Z=CB, TW=M, TS=M + 144, TP=[4, 240], QR=Q, QQ=7 * CAP, E=[4, 50], ONE=128,
+             TMPA=128, BLK=[8, 16], TRI=128, TRC=128, BLKP=[8, 16], B3=[3, 8, 16], IDN=128, WS=576, OH=192, XE=192,
+             G0=64, CMP=4 * CAP, CMQ=4 * CAP, ANS=3 * CAP, AL=4 * CAP, CT=[3, 64], CI=256, CZ=256, CO=256,
+             IB=128, YB=Q, IO=192, BIGT=64, S16=4, CW=8),
+    F32: dict(QXF=64, QF=48, QS=48, FL=192, CN=192, CN3=96, PC=48, QT=3 * CAP, GA=2 * CAP, KC=24, GR=16, TWO=8,
+              GT=16, D=12, I4=4, SM=32, PENA=64, PENU=64, LS=408, AT=64, PG=576, P2=576),
+    I32: dict(PM=192, TB=240, QI=96, QX=[2, 2, 16], IP=8, I12=12, SE=8, XT=16, WI=64, WJ=64, IC=64),
+    U16: dict(PMU=192, POS=48, U12=12, P2U=36, RU=8, O1=64, O2=64, O3=64, UC=64),
 }
 SCRATCH = {_n: ("sbuf", [128] + (_c if isinstance(_c, list) else [_c]), _d) for _d in _S for _n, _c in _S[_d].items()}
 for _b in range(8):
     SCRATCH["ps%d" % _b] = ("psum", [128, 512], F32)
 
-SEMAPHORES = ["V", "S", "P", "G", "sent", "q0", "q1", "q2", "ans", "last"] + ["d%d" % _i for _i in range(24)]
+SEMAPHORES = ["V", "S", "P", "G", "sent", "q0", "q1", "q2", "ans", "last"] + ["d%d" % _i for _i in range(32)]
 
 
 def rank_program(g, core, T, topo):
@@ -29,24 +54,26 @@ def rank_program(g, core, T, topo):
     N = len(T.cores)
     queue = {"V": g.vector, "S": g.scalar, "P": g.tensor, "G": g, "Y": g.sync}
     V, S, P = g.vector, g.scalar, g.tensor
-    ops, state, ndma, nsent = [], {}, [0], [0]
+    ops, state, ndma, nsent, step = [], {}, [0], [0], ["load"]
 
-    def op(eng, fn, r="", w="", dma=False):
-        me = {"eng": eng, "fn": fn, "deps": [], "dma": None, "used": False, "ext": None}
+    def now(name):
+        step[0] = name
+
+    def op(eng, fn, r, w, ns, lag=0, dma=False):
+        me = {"eng": eng, "fn": fn, "deps": [], "after": [], "dma": None, "used": False, "ext": None, "ns": ns, "lag": lag,
+              "w": w, "step": step[0]}
         if dma:
             me["dma"] = "d%d" % ndma[0]
             ndma[0] += 1
         for k in r.split():
-            st = state.setdefault(k, {"w": None, "r": []})
-            if st["w"] is not None:
-                me["deps"].append(st["w"])
+            st = state[k]
+            me["deps"].append(st["w"])
             if k.startswith("ps"):
                 me["deps"] += [o for o in st["r"] if o["eng"] != eng]
         for k in w.split():
             st = state.setdefault(k, {"w": None, "r": []})
             for o in ([st["w"]] if st["w"] is not None else []) + st["r"]:
-                if not (eng == "P" and o["eng"] == "P"):
-                    me["deps"].append(o)
+                me["after" if k[0] == "_" or eng == o["eng"] == "P" else "deps"].append(o)
         for k in r.split():
             state[k]["r"].append(me)
         for k in w.split():
@@ -54,342 +81,457 @@ def rank_program(g, core, T, topo):
         for o in me["deps"]:
             o["used"] = True
         ops.append(me)
+        return me
 
-    def landing(key, sem, val):
-        state[key] = {"w": {"eng": None, "dma": None, "ext": (sem, val), "used": True}, "r": []}
+    def landing(key, sem, val, like, lag):
+        me = {"eng": None, "dma": None, "ext": (sem, val), "used": True, "deps": [], "after": [like], "ns": 0, "lag": lag,
+              "step": step[0]}
+        ops.append(me)
+        state[key] = {"w": me, "r": []}
 
-    def ts(out, in0, s1, s2, op0, op1, r, w):
-        if op1 is None:
-            op("V", lambda: V.tensor_scalar(out, in0, s1, None, op0), r, w)
-        else:
-            op("V", lambda: V.tensor_scalar(out, in0, s1, s2, op0, op1), r, w)
+    def vec(fn, r, w, n):
+        return op("V", fn, r, w, max(n, 64) * CYC)
 
-    def t1(out, in0, s1, op0, r, w):
-        ts(out, in0, s1, None, op0, None, r, w)
+    def ts(out, in0, s1, s2, op0, op1, r, w, n=64):
+        vec(lambda: V.tensor_scalar(out, in0, s1, s2, op0, op1), r, w, n)
 
-    def tt(out, in0, in1, o, r, w):
-        op("V", lambda: V.tensor_tensor(out, in0, in1, o), r, w)
+    def t1(out, in0, s1, op0, r, w, n=64):
+        vec(lambda: V.tensor_scalar(out, in0, s1, None, op0), r, w, n)
 
-    def cp(out, in_, r, w):
-        op("V", lambda: V.tensor_copy(out, in_), r, w)
+    def tt(out, in0, in1, o, r, w, n=64):
+        vec(lambda: V.tensor_tensor(out, in0, in1, o), r, w, n)
 
-    def ms(ap, c, w):
-        op("V", lambda: V.memset(ap, c), "", w)
+    def cp(out, in_, r, w, n=64):
+        return vec(lambda: V.tensor_copy(out, in_), r, w, n)
 
-    def scan(out, d0, d1, init, op1, r, w):
-        op("V", lambda: V.tensor_tensor_scan(out, d0, d1, init, A.mult, op1), r, w)
+    def ms(ap, c, w, n=64):
+        vec(lambda: V.memset(ap, c), "", w, n)
 
-    def act(out, in_, f, r, w, **kw):
-        op("S", lambda: S.activation(out, in_, f, **kw), r, w)
+    def scan(out, d0, d1, init, op0, op1, r, w, n=64):
+        return vec(lambda: V.tensor_tensor_scan(out, d0, d1, init, op0, op1), r, w, n)
+
+    def act(out, in_, f, r, w, n=8, **kw):
+        op("S", lambda: S.activation(out, in_, f, **kw), r, w, 65 + n * CYC)
 
     def lin(out, in_, scale, bias, r, w):
         act(out, in_, AF.Identity, r, w, scale=scale, bias=bias)
 
-    def move(eng, out, in_, r, w):
+    def move(eng, out, in_, r, w, n):
         if eng == "S":
-            act(out, in_, AF.Copy, r, w)
+            act(out, in_, AF.Copy, r, w, n)
         else:
-            cp(out, in_, r, w)
+            cp(out, in_, r, w, n + 60)
 
-    def mm(items, r, w):
+    def mm(items, r, w, n=64):
         def fn():
             last = None
             for (o, l, rh, st, sp) in items:
                 last = P.matmul(o, l, rh, st, sp)
             return last
-        op("P", fn, r, w)
+        op("P", fn, r, w, len(items) * max(n, 64) * CYC)
 
-    def dma(eng, out, in_, r, w):
-        op(eng, lambda: queue[eng].dma_start(out, in_), r, w, dma=True)
+    def dma(eng, out, in_, r, w, lag=LOCAL):
+        op(eng, lambda: queue[eng].dma_start(out, in_), r, w + " _" + eng, 60, lag, True)
 
-    def iota(out, pattern, base, cm, w, flag=True):
+    def iota(out, pattern, base, cm, w, n, flag=True):
         if flag:
-            op("G", lambda: g.iota(out, pattern, base, cm, allow_small_or_imprecise_dtypes=True), "", w)
+            op("G", lambda: g.iota(out, pattern, base, cm, allow_small_or_imprecise_dtypes=True), "", w, 130 + 2 * n * CYC)
         else:
-            op("G", lambda: g.iota(out, pattern, base, cm), "", w)
+            op("G", lambda: g.iota(out, pattern, base, cm), "", w, 130 + 2 * n * CYC)
 
-    def sel(out, in_, pattern, cmp, base, cm, r, w):
-        op("G", lambda: g.affine_select(out, in_, pattern, cmp, 0.0, base, cm), r, w)
+    def zero(out, w, n):
+        iota(out, [[0, n]], 0, 0, w, n)
 
-    def send(dst_rank, out, in_, sem, r):
+    def sel(out, in_, pattern, cmp, base, cm, r, w, n=128):
+        op("G", lambda: g.affine_select(out, in_, pattern, cmp, 0.0, base, cm), r, w, 170 + 2 * n * CYC)
+
+    def send(dst_rank, out, in_, sem, r, w):
         dst = T.cores[dst_rank]
         rid, pid = topo.addr(dst, core)
         mask = topo.mask(core, dst)
         nsent[0] += len(topo.engines(core, dst))
-        op("G", lambda: g.remote_dma(out, in_, T.sem[sem], T.sem.sent, pid, rid, mask), r, "")
+        return op("G", lambda: g.remote_dma(out, in_, T.sem[sem], T.sem.sent, pid, rid, mask), r, w, 500)
 
     def shared(src):
-        sets = [topo.engines(T.cores[src], T.cores[o]) for o in range(N) if o != src]
+        sets = [topo.engines(T.cores[src], T.cores[o]) for o in range(src + 1, N)]
         return [e for e in sets[0] if all(e in s for s in sets)]
 
     ps = [T["ps%d" % b] for b in range(8)]
     KC = T.KC
     col = lambda j: KC[:, j:j + 1]
-    cK, cD1, cD0, cWB, cPW, cSC, cS0, cBA, cNK, cM7, cT1, cT2, cK1 = range(13)
+    cK, cWB, cPW, cSC, cBA, cNK, cM7, cT1, cT2, cK1, cWA = range(11)
 
     def slide(x, m):
         return T.WS[:, 144 * x + 15 - m:144 * x + 143 - m]
-    WP, WI_, WA, WB, W1 = range(5)
+    W1, WI_, WA, WB = range(4)
     wcol = lambda x: T.WS[:, 144 * x + 15:144 * x + 143:16]
 
     def sums(b, c0, x, src, lo, hi, start, stop, r):
         out = ps[b][:, c0:c0 + (hi - lo) // 16]
         mm([(out, slide(x, m), src[:, lo + m:hi:16], start and m == 0, stop and m == 15) for m in range(16)],
-           "WS%d %s" % (x, r), "ps%d" % b)
+           "WS%d %s" % (x, r), "ps%d" % b, (hi - lo) // 16)
 
-    others = [(rank + 1 + b) % N for b in range(N - 1)]
-    for b in range(N - 1):
-        landing("QL%d" % b, "q%d" % b, len(topo.engines(T.cores[others[b]], core)))
-    landing("ALr", "ans", sum(len(topo.engines(T.cores[o], core)) for o in others))
-    landing("Lr", "last", sum(len(shared(o)) for o in others if o < N - 1))
+    R3, R4 = 3 * CAP, 4 * CAP
+    QW = lambda a, b: T.QQ[:, R3 + a:R3 + b]
+    XS = lambda a, b: T.BUF[:, a:b]
+    names = lambda k, js: " ".join("%s%d" % (k, j) for j in js)
 
-    dma("Y", T.QB[:, 0:48], T.qt[:], "", "QBt")
-    dma("S", T.QB[:, 48:96], T.qi[:], "", "QBi")
-    dma("Y", T.TB[:], T.times[:], "", "TB")
-    dma("S", T.PM[:], T.pm[:], "", "PM")
-    dma("S", T.SE[:, 0:4], T.starts[:, 0:64], "", "SEs")
-    dma("S", T.SE[:, 4:8], T.starts[:, 1:65], "", "SEe")
-    dma("Y", T.X[:], T.x[:], "", "X")
+    for b in range(2):
+        for h in range(2):
+            dma("YS"[h], T.QX[:, b, h, :], T.qt[h:8:2, 256 * b:256 * b + 512], "", "QX%d%d" % (b, h), LOCAL + 400)
+    dma("Y", T.TB[:, 192:240], T.qt[:], "", "QB", LOCAL + 700)
+    dma("S", T.QI[:, 0:48], T.qi[:], "", "QI", LOCAL + 800)
+    dma("S", T.TB[:, 0:192], T.times[:], "", "TB", LOCAL + 1100)
+    dma("Y", T.PM[:], T.pm[:], "", "PM", LOCAL + 1300)
+    dma("S", T.SE[:, 0:4], T.starts[:, 0:64], "", "SEs", LOCAL + 1500)
+    dma("Y", T.SE[:, 4:8], T.starts[:, 1:65], "", "SEe", LOCAL + 1600)
+    dma("Y", T.X[:], T.x[:], "", "X", LOCAL + 3200)
 
-    ms(T.C16[:], 1.0 / 16, "C16")
-    ms(T.CM16[:], -1.0 / 16, "CM16")
-    ms(T.QW[:], 0.0, "QW")
+    nload = len(ops)
     ms(T.ONE[:], 1.0, "ONE")
-    iota(T.IP[:, 0:1], [[0, 1]], 0, 1, "IP0", False)
-    iota(T.IO[:], [[0, 12], [1, 16]], 0, 0, "IO")
-    grp, neg = [[-16, 8], [0, 16]], [[16, 8], [0, 16]]
-    sel(T.TMPA[:], T.C16[:], grp, A.is_ge, 0, 1, "C16", "TMPA")
-    sel(T.TMPB[:], T.CM16[:], [[-16, 8], [-1, 16]], A.is_gt, 0, 1, "CM16", "TMPB")
+    ms(T.TW[:, 0:1024], 0.0, "TWz0", 512)
+    ms(T.E[:, :, 1], 0.0, "Ez")
+    move("S", T.QR[:], T.TW[:, 0:Q], "TWz0", "QRz", Q)
+    move("S", QW(0, R4), T.TW[:, 0:R4], "TWz0", "QW", R4)
+    move("S", T.TW[:, 1024:2048], T.TW[:, 0:1024], "TWz0", "TWz1", 1024)
+    zero(T.TW[:, 2048:M], "TWz2", 1024)
+    iota(T.TWO[:], [[0, 8]], 2, 0, "TWO", 8)
+    iota(T.GR[:, 0:8], [[0, 8]], 256, 0, "GRa", 8)
+    zero(T.LS[:, 192:208], "L2z", 16)
+    iota(T.IP[:, 0:1], [[0, 1]], 0, 1, "IP0", 1, False)
+    iota(T.I4[:], [[16, 4]], DUMP, 0, "I4", 4)
+    for b in range(N):
+        act(T.FL[:, 48 * b:48 * b + 48], T.ONE[:, 0:48], AF.Copy, "ONE", "FL%d" % b, 48, scale=CAP * b - 1.0)
+    iota(T.IO[:], [[0, 12], [1, 16]], 0, 0, "IO", 192)
+    iota(T.I12[:], [[1, 12]], 0, 0, "I12", 12, False)
+    act(T.BIGT[:], T.ONE[:, 0:64], AF.Copy, "ONE", "BIGT", 64, scale=BIG)
+    grp, neg, lo8, hi8 = [[-16, 8], [0, 16]], [[16, 8], [0, 16]], [[0, 8], [-1, 16]], [[0, 8], [1, 16]]
+    sel(T.TMPA[:], T.ONE[:, 0:128], grp, A.is_ge, 0, 1, "ONE", "TMPA")
     sel(T.BLK[:], T.TMPA[:], neg, A.is_ge, 15, -1, "TMPA", "BLK")
-    sel(T.TRI[:], T.TMPB[:], neg, A.is_ge, 15, -1, "TMPB", "TRI")
-    iota(T.CR[0:1, :], [[CAP // 16, 4], [0, 48]], 0, 0, "CR")
-    iota(T.I9[:], [[1, 9]], 0, 0, "I9")
-    iota(T.I12[:], [[1, 12]], 0, 0, "I12", False)
-    iota(T.D[:], [[1, 4]], M, 4, "D")
-    iota(T.WS[:], [[0, 720]], 0, 0, "WSz")
-    iota(T.CW[:, 0:16], [[48, 2], [0, 8]], 16, 0, "CW")
-    sel(T.TMPC[:], T.ONE[:], grp, A.is_ge, 0, 1, "ONE", "TMPC")
-    sel(T.CW[:, 16:24], T.CW[:, 8:16], [[-16, 8]], A.is_ge, 0, 1, "CW", "CWb")
-    sel(wcol(WP), T.TMPC[:, 0:128:16], [[16, 8]], A.is_ge, 2, -1, "TMPC WSz", "WS0")
-    iota(T.B3[:], [[0, 384]], 0, 0, "B3z")
-    sel(T.BLKP[:], T.TMPC[:], neg, A.is_ge, 2, -1, "TMPC", "BLKP")
-    sel(wcol(WI_), T.CW[:, 0:8], [[-16, 8]], A.is_equal, -3, 1, "CW WSz", "WS1")
-    sel(wcol(WA), T.CW[:, 16:24], [[16, 8]], A.is_ge, 7, -1, "CWb WSz", "WS2")
-    sel(wcol(W1), T.TMPC[:, 0:128:16], [[16, 8]], A.is_ge, 15, -1, "TMPC WSz", "WS4")
-    iota(T.TS[:, M:M + 144], [[0, 144]], 0, 0, "TSz")
-    iota(T.CT[:, 0:64], [[0, 64]], 0, 0, "CT0")
-    iota(T.F[:, 0:16], [[0, 16]], 0, 0, "Fz")
-    iota(T.L2[:, 192:208], [[0, 16]], 0, 0, "L2z")
-    move("S", T.QR[:], T.QW[:, 0:Q], "QW", "QRz")
-    for h in range(3):
-        move("S", T.TW[:, 1024 * h:1024 * h + 1024], T.QW[:, 0:1024], "QW", "TWz%d" % h)
-    ms(T.RST[:], 1.0, "RST")
-    ms(T.TWO[:], 2.0, "TWO")
-    t1(T.IP[:, 1:2], T.IP[:, 0:1], 15, A.bitwise_and, "IP0", "IP1")
-    ts(T.IP[:, 2:3], T.IP[:, 0:1], 4, 1, A.arith_shift_right, A.bitwise_and, "IP0", "IP2")
-    ms(T.GR[:, 0:8], 512.0, "GRa")
-    ms(T.RST[:, 0:192:48], 0.0, "RST")
-    cp(KC[:, 0:2], T.IP[:, 1:3], "IP1 IP2", "cK")
-    scan(T.GR[:, 8:16], T.TWO[:], T.TWO[:], 1.0, A.max, "TWO", "GRb")
-    ts(T.OH[:], T.IO[:], col(cK), 16.0, A.is_equal, A.mult, "IO cK", "OH")
-    t1(col(cM7), col(cK), 7.0, A.is_le, "cK", "cM7")
-    lin(col(cD0), col(cD1), -1.0, 1.0, "cK", "cD0")
-    lin(col(cT1), col(cK), -1.0 / 16, 239.0 / 256, "cK", "cT1")
-    lin(col(cK1), col(cK), BIG, BIG, "cK", "cK1")
-    lin(col(cNK), col(cK), -BIG, 0.0, "cK", "cNK")
-    lin(col(cT2), col(cM7), -65280.0, 0.0, "cM7", "cT2")
-    lin(col(cBA), col(cT1), col(cM7), -0.5 + 1.0 / 512, "cT1 cM7", "cBA")
-    lin(T.PB[:], T.I9[:], 16.0 * BIG, col(cK1), "I9 cK1", "PB")
-
-    masks = (0x3F8000, 0x7F80, 0x7F)
-    for j in range(3):
-        t1(T.QI3[:, 48 * j:48 * j + 48], T.QB[:, 0:48], masks[j], A.bitwise_and, "QBt", "QI%d" % j)
-    t1(T.QS[:], T.QB[:, 0:48], 20, A.arith_shift_right, "QBt", "QS")
-    t1(T.QH[:], T.QB[:, 48:96], 2, A.arith_shift_right, "QBi", "QH")
-    cp(T.QP[:, 0:144], T.QI3[:], "QI0 QI1 QI2", "QP")
-    t1(T.QF[:], T.QH[:], -63.0 / 16, A.mult, "QH", "QF")
-    for s in range(N):
-        t1(T.E[:, 48 * s:48 * s + 48], T.QS[:], float(s), A.is_equal, "QS", "E%d" % s)
-        if s == 0:
-            tt(T.QP[:, 144:192], T.QB[:, 48:96], T.QF[:], A.add, "QBi QF", "QP3")
-    for j in range(3):
-        dma("Y", T.QR[j:128:16, :], T.QP[:, 48 * j:48 * j + 48], "QP QRz", "QR%d" % j)
-    dma("Y", T.QR[3:128:16, :], T.QP[:, 144:192], "QP3 QRz", "QR3")
-    Es = "E0 E1 E2 E3"
-    mm([(ps[0][:, 0:192], T.BLK[:], T.E[:], True, True)], "BLK " + Es, "ps0")
-    mm([(ps[1][:, 0:192], T.TRI[:], T.E[:], True, False),
-        (ps[1][:, 0:192], T.ONE[0:1, :], T.CR[0:1, :], False, True)], "TRI ONE CR " + Es, "ps1")
-    for j in range(3):
-        t1(T.TI3[:, 192 * j:192 * j + 192], T.TB[:], masks[j], A.bitwise_and, "TB", "TI%d" % j)
-    scan(T.CN[:], T.RST[:], ps[0][:, 0:192], 0.0, A.add, "RST ps0", "CN")
-    cp(T.TP[:], T.TI3[:], "TI0 TI1 TI2", "TP")
-    for j in range(3):
-        dma("Y", T.TW[j:128:16, :], T.TP[:, 192 * j:192 * j + 192], "TP TWz0 TWz1 TWz2", "TW%d" % j)
-    tt(T.CN2[:], T.CN[:], ps[1][:, 0:192], A.add, "CN ps1", "CN2")
-    cp(T.PMU[:], T.PM[:], "PM", "PMU")
-    tt(T.CN[:], T.CN2[:], T.E[:], A.mult, "CN2 " + Es, "CN")
-    ts(T.QF2[:], T.QS[:], 4.0, 1.0 / 16, A.mult, A.add, "QS", "QF2")
-    tt(T.CN3[:], T.CN[:, 0:96], T.CN[:, 96:192], A.add, "CN", "CN3")
-    tt(T.PC[:, 3:6, :], T.QF2[:], T.QP[:, 144:192], A.add, "QF2 QP3", "PC1")
-    tt(T.PC[:, 0:3, :], T.CN3[:, 0:48], T.CN3[:, 48:96], A.add, "CN3", "PC0")
-    t1(T.TI[:, :, 0, :], T.PC[:], col(cD0), A.mult, "PC0 PC1 cD0", "TIa")
-    t1(T.TI[:, :, 1, :], T.PC[:], col(cD1), A.mult, "PC0 PC1 cK", "TIb")
-    op("V", lambda: V.transpose(T.TO[:], T.TI[:]), "TIa TIb", "TO")
-    tt(T.R[:], T.TO[:, :, 0, :], T.TO[:, :, 1, :], A.add, "TO", "R")
-    for u in range(3):
-        ts(T.POS[:, u:96:3], T.R[:, u:6:3, :], 16.0, -1.0, A.mult, A.add, "R", "POS%d" % u)
-    POS = "POS0 POS1 POS2"
-    cp(T.QW[:, :].indirect(T.POS[:, 0:48]), T.QR[:], POS + " QR0 QR1 QR2 QR3", "QW")
-    for b in range(N - 1):
-        d = others[b]
-        slot = (rank - d - 1) % N
-        send(d, T.QL[:, CAP * slot:CAP * slot + CAP], T.QW[:, CAP * d:CAP * d + CAP], "q%d" % slot, "QW")
-
-    def order(eng, dst, src, a, b, r, w):
-        move(eng, dst[:, a:b], src[:, :].indirect(T.PMU[:, a // 16:b // 16]), "PMU " + r, w)
-
-    def times(h):
-        order("S", T.TS, T.TW, 1024 * h, 1024 * h + 1024, "TW0 TW1 TW2", "TS%d" % h)
-        sums(4, 64 * h, WP, T.TS, 1024 * h, 1024 * h + 1024, True, True, "TS%d" % h)
-    order("S", T.XS, T.X, 0, 1024, "X", "XS0")
-    order("S", T.XS, T.X, 1024, 2048, "X", "XS1")
-    times(0)
-    act(T.B3[:, 0, :, 0:8], T.BLK[:, :, 0:8], AF.Copy, "BLK B3z", "B30", scale=2.0)
-    act(T.B3[:, 1, :, 8:16], T.BLK[:, :, 8:16], AF.Copy, "BLK B3z", "B31", scale=2.0)
-    order("S", T.XS, T.X, 2048, 2560, "X", "XS2")
-    own, R3 = CAP * rank, 3 * CAP
-    mm([(ps[2][:, 0:CAP], T.BLKP[:], T.QW[:, own:own + CAP], True, True)], "BLKP QW", "ps2")
-    sums(6, 0, WI_, T.QW, own, own + CAP, True, True, "QW")
-
-    SM = T.SM
-    c0f, n16, ne, c1, e15, sd = [SM[:, 4 * j:4 * j + 4] for j in range(6)]
-    t1(T.C0[:], T.SE[:, 0:4], 4, A.arith_shift_right, "SEs", "C0")
-    cp(T.SF[:], T.SE[:], "SEs SEe", "SF")
+    sel(T.TRI[:], T.TMPA[:], [[1, 128]], A.is_ge, 0, -1, "TMPA", "TRI")
+    sel(T.TRC[:], T.BLK[:], [[-1, 128]], A.is_gt, 0, 1, "BLK", "TRC")
+    sel(T.BLKP[:], T.TMPA[:], neg, A.is_ge, 2, -1, "TMPA", "BLKP")
+    sel(T.B3[:, 0], T.BLK[:], lo8, A.is_ge, 7, 0, "BLK", "B30")
+    sel(T.B3[:, 1], T.BLK[:], hi8, A.is_ge, -8, 0, "BLK", "B31")
+    sel(T.IDN[:], T.ONE[:], [[-1, 128]], A.is_equal, 0, 1, "ONE", "IDN")
+    zero(T.WS[:], "WSz", 576)
+    iota(T.CW[:], [[0, 8]], 16, 0, "CW", 8)
+    sel(wcol(WI_), T.CW[:], [[-16, 8]], A.is_equal, -3, 1, "CW WSz", "WS1", 8)
+    sel(wcol(W1), T.TMPA[:, 0:128:16], [[16, 8]], A.is_ge, 15, -1, "TMPA WSz", "WS0", 8)
+    zero(T.TS[:, M:M + 144], "TSz", 144)
+    zero(T.Z[:, M:CB], "Zz", 96)
+    if rank < N - 1:
+        zero(XS(FB + M, FB + M + 95), "Fz", 95)
+    zero(XS(CB + 1024, FB), "CRb", 1)
+    if rank == 0:
+        for h in range(2):
+            zero(XS(CB + 512 * h, CB + 512 * h + 512), "CR%d" % h, 512)
+    else:
+        iota(T.IC[:], [[rank + 1, 64]], rank - 1, 0, "IC", 64, False)
+        cp(T.UC[:], T.IC[:], "IC", "UC")
+        zero(XS(M, CB), "XSz", 96)
+        zero(T.CZ[:, 0:NI * (rank + 1):rank + 1], "CZz", 64)
+    t1(T.IP[:, 4:5], T.IP[:, 0:1], 15, A.bitwise_and, "IP0", "IP1")
+    scan(T.GR[:, 8:16], T.TWO[:], T.LS[:, 192:200], 8.0, A.mult, A.add, "TWO L2z", "GRb")
+    cp(KC[:, 0:1], T.IP[:, 4:5], "IP1", "cK")
     cp(T.U12[:], T.I12[:], "I12", "U12")
-    cp(c0f, T.C0[:], "C0", "c0f")
-    tt(ne, T.SF[:, 4:8], T.SF[:, 0:4], A.is_gt, "SF", "ne")
+    ts(T.OH[:], T.IO[:], col(cK), -BIG, A.is_equal, A.mult, "IO cK", "OH", 96)
+    lin(T.D[:, 0:4], T.I4[:], 1.0, col(cK), "I4 cK", "D")
+    lin(T.D[:, 8:12], T.D[:, 0:4], -16.0, 16.0 * (DUMP + NI), "D", "DK")
+    nconst = len(ops)
+    now("power")
+    t1(col(cM7), col(cK), 7.0, A.is_le, "cK", "cM7")
     tt(T.GT[:], T.GR[:], T.OH[:, 0:16], A.mult, "GRa GRb OH", "GT")
-    t1(n16, c0f, -16.0, A.mult, "c0f", "n16")
-    t1(c1, c0f, 1.0, A.add, "c0f", "c1")
-    op("V", lambda: V.tensor_reduce(col(cPW), T.GT[:], AxisListType.X, A.add), "GT", "cPW")
-    tt(T.XT[:, 0:4], T.SF[:, 4:8], n16, A.add, "SF n16", "XT0")
-    tt(T.XT[:, 4:8], T.SF[:, 0:4], n16, A.add, "SF n16", "XT1")
-    tt(T.XT[:, 8:12], c1, ne, A.mult, "c1 ne", "XT2")
-    for c in range(4):
-        t1(T.P2L[:, c:36:4], T.I9[:], SM[:, c:c + 1], A.add, "I9 c0f", "P2L%d" % c)
-    tt(T.XE[:], T.XT[:, 0:12].indirect(T.U12[:, 0:12]), T.OH[:], A.mult, "XT0 XT1 XT2 U12 OH", "XE")
-    mm([(ps[3][:, 0:64], T.B3[:, 0], T.XE[:, 0:64], True, False),
-        (ps[3][:, 0:64], T.B3[:, 1], T.XE[:, 128:192], False, True)], "B30 B31 XE", "ps3")
-    mm([(ps[7][:, 0:128], T.BLK[:], T.XE[:, 0:128], True, True)], "BLK XE", "ps7")
-    times(1)
-    times(2)
-    P2L = "P2L0 P2L1 P2L2 P2L3"
-    op("V", lambda: V.reciprocal(col(cS0), col(cPW)), "cPW", "cS0")
-    t1(T.G1U[:, 4:36], T.P2L[:, 4:36], 16.0, A.mult, P2L, "G1Ua")
-    cp(T.G1U[:, 0:4], T.SF[:, 0:4], "SF", "G1Ub")
-    tt(sd, T.SF[:, 0:4], T.D[:], A.subtract, "SF D", "sd")
-    cp(T.P2U[:], T.P2L[:], P2L, "P2U")
-    t1(col(cSC), col(cS0), 16.0, A.mult, "cS0", "cSC")
-    tt(sd, sd, ne, A.mult, "sd ne", "sd")
-    t1(e15, T.SF[:, 4:8], 15.0, A.add, "SF", "e15")
-    t1(T.Z[:, 0:2048], T.XS[:, 0:2048], 0.0, A.is_equal, "XS0 XS1", "Z0")
-    tt(sd, sd, T.D[:], A.add, "sd D", "sd")
-    tt(e15, e15, ne, A.mult, "e15 ne", "e15")
-    order("V", T.XS, T.X, 2560, M, "X", "XS3")
-    cp(T.RU[:], sd, "sd", "RU")
-    ts(T.WI[:], ps[3][:, 0:64], col(cSC), col(cBA), A.mult, A.add, "ps3 cSC cBA", "WI")
-    t1(T.Z[:, 2048:M], T.XS[:, 2048:M], 0.0, A.is_equal, "XS2 XS3", "Z1")
-    t1(T.WJ[:], T.WI[:], 1, A.bitwise_and, "WI", "WJ")
-    cp(T.O1[:, 48:64], ps[6][:, 0:16], "ps6", "O1o")
-    cp(T.Z[:, :].indirect(T.RU[:, 0:4]), T.CT[:, 0:64], "RU CT0", "Z0 Z1")
-    ts(T.PENA[:], T.WJ[:], -BIG, BIG, A.mult, A.add, "WJ", "PENA")
-    cp(T.LU[:], e15, "e15", "LU")
-
-    move("S", T.B3[:, 2, :, 8:16], T.BLKP[:, :, 8:16], "BLKP B3z", "B32")
-    move("S", T.G1[:], T.TS[:, :].indirect(T.G1U[:, 0:36]), "TS0 TS1 TS2 TSz G1Ua G1Ub", "G1")
-    mm([(ps[3][:, 0:64], T.B3[:, 2], T.G1[:, 0:64], True, False)]
-       + [(ps[3][:, 0:64], slide(WP, k), T.G1[:, 64 * k + 64:64 * k + 128], False, k == 7) for k in range(8)],
-       "B32 WS0 G1", "ps3")
-    move("S", T.QT[:, R3:R3 + CAP], ps[2][:, 0:CAP], "ps2", "QT3")
-    lin(col(cWB), col(cPW), 8.0, col(cT2), "cPW cT2", "cWB")
-    move("S", T.L2[:, 0:192], ps[4][:, 0:192], "ps4", "L2")
+    vec(lambda: V.tensor_reduce(col(cPW), T.GT[:], AxisListType.X, A.add), "GT", "cPW", 64)
+    vec(lambda: V.reciprocal(col(cSC), col(cPW)), "cPW", "cSC", 220)
+    now("scales")
+    lin(col(cT1), col(cK), -1.0 / 16, 239.0 / 256, "cK", "cT1")
+    lin(col(cBA), col(cT1), col(cM7), -0.5 + 1.0 / 512, "cT1 cM7", "cBA")
+    lin(col(cT2), col(cM7), -240.0, 0.0, "cM7", "cT2")
+    lin(col(cWA), col(cM7), 64.0, 0.0, "cM7", "cWA")
+    now("weights")
+    lin(col(cWB), col(cPW), -1.0 / BIG, col(cT2), "cPW cT2", "cWB")
+    act(wcol(WA), T.BLK[:, :, 0], AF.Copy, "BLK WSz cWA", "WS2", scale=col(cWA))
     act(wcol(WB), T.BLK[:, :, 0], AF.Copy, "BLK WSz cWB", "WS3", scale=col(cWB))
 
-    scan(T.F[:, 16:16 + M], T.Z[:, 0:M], T.XS[:], 0.0, A.add, "Z0 Z1 XS0 XS1 XS2 XS3", "F")
-    lcol = (64, 256, 320)
+    now("slot")
+    ts(T.QXF[:], T.QX[:], 0.5 - 2.0 ** 19, RND, A.add, A.add, "QX00 QX01 QX10 QX11", "QXF")
+    vec(lambda: V.transpose(T.QS[:, 16:48], T.QXF[:, 32:64]), "QXF", "QS", 64)
+    vec(lambda: V.transpose(T.QS[:, 0:32], T.QXF[:, 0:32]), "QXF", "QS", 64)
+    for b in range(N):
+        t1(T.E[:, b, 2:50], T.QS[:], RND + 2.0 ** 20 * ((rank + b) % N), A.is_equal, "QS Ez", "E%d" % b)
+    Es = names("E", range(N))
+    mm([(ps[0][:, 0:192], T.TRI[:], T.E[:, :, 2:50], True, False),
+        (ps[0][:, 0:192], T.TRC[:], T.E[:, :, 1:49], False, True)], "TRI TRC " + Es, "ps0", 192)
+    def pieces(bank, a, b, r, w):
+        mid, key = ps[bank][:, 0:b - a], "ps%d" % bank
+        ts(T.TP[:, 0, a:b], T.TB[:, a:b], R14, R14, A.add, A.subtract, r, w + "0", b - a)
+        ts(mid, T.TB[:, a:b], R7, R7, A.add, A.subtract, r, key, b - a)
+        tt(T.TP[:, 1, a:b], mid, T.TP[:, 0, a:b], A.subtract, "%s %s0" % (key, w), w + "1", b - a)
+        tt(T.TP[:, 2, a:b], T.TB[:, a:b], mid, A.subtract, "%s %s" % (key, r), w + "2", b - a)
+    now("qpieces")
+    pieces(3, 192, 240, "QB", "QP")
+    t1(T.QI[:, 48:96], T.QI[:, 0:48], 2, A.arith_shift_right, "QI", "QH")
+    t1(T.QF[:], T.QI[:, 48:96], -63.0 / 16, A.mult, "QH", "QF")
+    tt(T.TP[:, 3, 192:240], T.QI[:, 0:48], T.QF[:], A.add, "QI QF", "QP3", 96)
+    for j in range(4):
+        dma("Y", T.QR[j:128:16, :], T.TP[:, j, 192:240], "QP%d QRz" % j, "QR%d" % j, LOCAL + 1200)
+    now("pmu")
+    cp(T.PMU[:], T.PM[:], "PM", "PMU", 192)
+    now("tpieces")
+    pieces(2, 0, 192, "TB", "TP")
+    for j in range(3):
+        dma("Y", T.TW[j:128:16, :], T.TP[:, j, 0:192], "TP%d TWz0 TWz1 TWz2" % j, "TW%d" % j, LOCAL + 200)
+    now("slot")
+    scan(ps[1][:, 0:192], T.FL[:], ps[0][:, 0:192], -1.0, A.max, A.add, names("FL", range(N)) + " ps0", "ps1", 192)
+    tt(T.CN[:], ps[1][:, 0:192], T.E[:, :, 2:50], A.mult, "ps1 " + Es, "CN", 192)
+    tt(T.CN3[:], T.CN[:, 0:96], T.CN[:, 96:192], A.add, "CN", "CN3", 192)
+    tt(T.PC[:], T.CN3[:, 0:48], T.CN3[:, 48:96], A.add, "CN3", "PC", 96)
+    cp(T.POS[:], T.PC[:], "PC", "POS")
 
-    for b in range(N - 1):
-        mm([(ps[b][:, 0:CAP], T.BLKP[:], T.QL[:, CAP * b:CAP * b + CAP], True, True)], "BLKP QL%d" % b, "ps%d" % b)
-        move("S", T.QT[:, CAP * b:CAP * b + CAP], ps[b][:, 0:CAP], "ps%d" % b, "QT%d" % b)
-    QLr, QTr = "QL0 QL1 QL2", "QT0 QT1 QT2"
-    sums(5, 0, WI_, T.QL, 0, R3, True, True, QLr)
-    tt(T.AT[:], ps[3][:, 0:64], T.PENA[:], A.add, "ps3 PENA", "AT")
-    cp(T.O1[:, 0:48], ps[5][:, 0:48], "ps5", "O1r")
-    sums(5, 64, WI_, T.QL, 0, R3, True, False, QLr)
-    act(T.PLO[:], ps[7][:, 64:128], AF.Relu, "ps7 cNK", "PLO", bias=col(cNK), scale=BIG)
-    for n in range(9):
-        act(T.PEN[:, 64 * n:64 * n + 64], ps[7][:, 0:64], AF.Relu, "ps7 PB", "PEN%d" % n, bias=T.PB[:, n:n + 1], scale=-BIG)
+    now("scatter")
+    cp(QW(0, R4).indirect(T.POS[:, :]), T.QR[:], "POS QR0 QR1 QR2 QR3", "QW", Q * SCATTER)
+    for b in range(1, N):
+        me = send((rank + b) % N, T.QQ[:, CAP * (b - 1):CAP * b], QW(CAP * b, CAP * b + CAP), "q%d" % (b - 1), "QW", "_q")
+        landing("QL%d" % (b - 1), "q%d" % (b - 1), len(topo.engines(T.cores[(rank - b) % N], core)), me, REMOTE + 600 + 250 * b)
+
+    s_, e_ = T.SE[:, 0:4], T.SE[:, 4:8]
+    r_ = T.XT[:, 4:8]
+    ln, big, dm, vv, ru, lu = [T.SM[:, 4 * j:4 * j + 4] for j in range(6)]
+    SEs, SEe = "SEs", "SEe"
+    now("bounds")
+    tt(ln, e_, s_, A.subtract, SEs + " " + SEe, "ln")
+    t1(r_, s_, 15, A.bitwise_and, SEs, "r")
+    t1(big, ln, 4096.0, A.mult, "ln", "big")
+    tt(T.S16[:], s_, r_, A.subtract, SEs + " r", "S16")
+    tt(T.XT[:, 0:4], ln, r_, A.add, "ln r", "XT0")
+    tt(vv, T.S16[:], T.D[:, 8:12], A.add, "S16 DK", "vv")
+    tt(T.XT[:, 8:12], vv, big, A.min, "vv big", "XT2")
+    tt(T.XE[:], T.XT[:, 0:12].indirect(T.U12[:, 0:12]), T.OH[:], A.mult, "XT0 r XT2 U12 OH", "XE", 360)
+
+    def plus16(out, n, src):
+        return [(out, T.ONE[0:16 * n, :], src[0:16 * n, :], False, False)] if n else []
+
+    def bound(out, xe, n):
+        return [(out, T.BLK[:], xe, True, False)] + plus16(out, n, T.BIGT) + [(out, T.TRI[:], T.BIGT[:], False, True)]
+    mm(sum([bound(ps[7][:, 64 * n:64 * n + 64], T.XE[:, 0:64], n) for n in range(8)], []), "BLK TRI ONE BIGT XE", "ps7")
+    mm(bound(ps[4][:, 64:128], T.XE[:, 0:64], 8) + bound(ps[4][:, 128:192], T.XE[:, 64:128], 0), "BLK TRI ONE BIGT XE", "ps4")
+    now("bits")
+    mm([(ps[4][:, 0:64], T.B3[:, 0], T.XE[:, 0:64], True, False),
+        (ps[4][:, 0:64], T.B3[:, 1], T.XE[:, 128:192], False, True)], "B30 B31 XE", "ps4")
+
+    now("cols")
+    mm([(ps[5][:, 0:4], T.IDN[:], T.S16[:], True, True)]
+       + sum([[(ps[5][:, 4 * n:4 * n + 4], T.IDN[:], T.S16[:], True, False),
+               (ps[5][:, 4 * n:4 * n + 4], T.ONE[0:16 * n, :], T.ONE[0:16 * n, 0:4], False, True)] for n in range(1, 9)], []),
+       "ONE IDN S16", "ps5")
+    t1(T.P2U[:], ps[5][:, 0:36], 1.0 / 16, A.mult, "ps5", "P2U")
+    now("lists")
+    tt(dm, T.D[:, 0:4], big, A.subtract, "D big", "dm")
+    tt(ru, s_, dm, A.max, SEs + " dm", "ru")
+    tt(lu, e_, dm, A.max, SEe + " dm", "lu")
+    cp(T.RU[:], T.SM[:, 16:24], "ru lu", "RU")
+
+    def order(eng, dst, src, a, b, r, w):
+        move(eng, dst[:, a:b], src[:, :].indirect(T.PMU[:, a // 16:b // 16]), "PMU " + r, w, (b - a) * GATHER)
+    nx, nt = range(len(XCUT) - 1), range(len(TCUT) - 1)
+    scut = [0] + [c // 16 - 8 for c in TCUT[1:-1]] + [193]
+
+    def firsts(h):
+        a, b = scut[h], scut[h + 1]
+        now("f%d" % h)
+        mm([(ps[3][:, a:b], slide(W1, k), T.TS[:, 16 * (a + k + 1):16 * (b + k) + 1:16], k == 0, k == 7)
+            for k in range(8)], "WS0 TSz " + names("TS", range(max(h - 1, 0), h + 1)), "ps3", b - a)
+
+    def turn(h):
+        now("u%d" % h)
+        sums(0, TCUT[h] // 16, W1, T.TS, TCUT[h], TCUT[h + 1], True, True, "TS%d" % h)
+
+    for h in nx:
+        a, b = XCUT[h], XCUT[h + 1]
+        now("x%d" % h)
+        order(XENG[h], T.BUF, T.X, a, b, "X", "XS%d" % h)
+        now("z%d" % h)
+        t1(T.Z[:, a:b], XS(a, b), 0.0, A.is_equal, "XS%d" % h, "Z%d" % h, (b - a) // 2)
+    for h in nt:
+        now("t%d" % h)
+        order(TENG[h], T.TS, T.TW, TCUT[h], TCUT[h + 1], "TW0 TW1 TW2", "TS%d" % h)
+        firsts(h)
+        turn(h)
+    XSa, Za = names("XS", nx), names("Z", nx)
+    now("fill")
+    me = cp(T.Z[:, :].indirect(T.RU[:, 0:4]), T.TS[:, M:M + 64], "RU TSz Zz", Za, 60 + 64 * SCATTER)
+    landing("Lr", "last", sum(len(shared(o)) for o in range(rank)), me, M // 2 * CYC + REMOTE + 900)
     if rank < N - 1:
-        mine = T.CT[:, lcol[rank]:lcol[rank] + NI]
-        move("S", mine, T.F[:, :].indirect(T.LU[:, 0:4]), "Fz F LU", "Lo")
-        ids = [topo.addr(T.cores[o], core) for o in others]
+        scan(XS(FB, FB + M), T.Z[:, 0:M], XS(0, M), 0.0, A.mult, A.add, Za + " " + XSa, "F", M // 2)
+        mine = T.CT[:, rank, :]
+        move("V", mine, XS(FB - 1, FB + M + 95).indirect(T.RU[:, 4:8]), "CRb Fz F RU", "Lo", 100)
+        ids = [topo.addr(T.cores[o], core) for o in range(rank + 1, N)]
         nsent[0] += len(shared(rank))
         op("G", lambda: g.remote_dma_fused(
             [RemoteDMATransfer(dst_ids=[DstId(rid=a[0], pnc=a[1]) for a in ids], dma_engine_mask=sum(1 << e for e in shared(rank)),
-                               remote_sem=T.sem["last"], srcs=[mine], dsts=[mine for a in ids])], local_sem=T.sem.sent), "Lo", "")
-    tt(T.CMP[:, 0:R3], T.AT[:, :].indirect(T.O1[:, 0:48]), T.QT[:, 0:R3], A.is_le, "AT O1r " + QTr, "CMPr")
-    sums(5, 64, WA, T.CMP, 0, R3, False, True, "CMPr")
-    sums(6, 0, WB, T.CMP, 0, R3, True, False, "CMPr")
-    tt(T.PEN[:, 0:64], T.PEN[:, 0:64], T.PLO[:], A.subtract, "PEN0 PLO", "PEN0")
-    tt(T.P2[:], T.L2[:, :].indirect(T.P2U[:, 0:36]), T.PEN[:], A.add,
-       "L2 L2z P2U " + " ".join("PEN%d" % n for n in range(9)), "P2")
-    cp(T.O2[:, 0:48], ps[5][:, 64:112], "ps5", "O2r")
-    tt(T.CMQ[:, 0:R3], T.P2[:, :].indirect(T.O2[:, 0:48]), T.QT[:, 0:R3], A.is_le, "P2 O2r " + QTr, "CMQr")
-    sums(6, 0, W1, T.CMQ, 0, R3, False, True, "CMQr")
-    tt(T.CMP[:, R3:R3 + CAP], T.AT[:, :].indirect(T.O1[:, 48:64]), T.QT[:, R3:R3 + CAP], A.is_le, "AT O1o QT3", "CMPo")
-    sums(4, 0, WI_, T.QW, own, own + CAP, True, False, "QW")
-    sums(4, 0, WA, T.CMP, R3, R3 + CAP, False, True, "CMPo")
-    sums(3, 0, WB, T.CMP, R3, R3 + CAP, True, False, "CMPo")
-    t1(T.O3[:, 0:48], ps[6][:, 0:48], -1.0, A.add, "ps6", "O3r")
-    for b in range(N - 1):
-        move("V" if b == 1 else "S", T.ANS[:, CAP * b:CAP * b + CAP], T.F[:, :].indirect(T.O3[:, 16 * b:16 * b + 16]),
-             "Fz F O3r", "ANS%d" % b)
-        send(others[b], T.AL[:, own:own + CAP], T.ANS[:, CAP * b:CAP * b + CAP], "ans", "ANS%d" % b)
+                               remote_sem=T.sem["last"], srcs=[mine], dsts=[mine for a in ids])], local_sem=T.sem.sent),
+           "Lo", "_l", 500, LAST)
 
-    L = "Lr Lo"
-    last = lambda s: T.CT[:, lcol[s]:lcol[s] + NI]
-    t1(T.CZ[:], T.CT[:, 256:384], 0.0, A.is_equal, L, "CZ")
-    tt(T.CY[:], T.CZ[:, 0:64], last(0), A.mult, "CZ " + L, "CY")
-    tt(T.CT[:, 128:192], T.CY[:], last(1), A.add, "CY " + L, "CT2")
-    tt(T.CY[:], T.CZ[:, 64:128], T.CT[:, 128:192], A.mult, "CZ CT2", "CY")
-    tt(T.CT[:, 192:256], T.CY[:], last(2), A.add, "CY " + L, "CT3")
-    cs = [slice(CAP * h, CAP * h + CAP) for h in range(3)]
-    move("S", T.CG[:], T.CT[:, 0:256].indirect(T.POS[:, 48:96]), "CT0 CT2 CT3 " + L + " " + POS, "CG")
-    for h in range(3):
-        move("S", ps[h][:, 0:CAP], T.CG[:, cs[h]], "CG", "ps%d" % h)
+    def spread(b):
+        bank, at = place_qt[b]
+        mm([(ps[bank][:, at:at + CAP], T.BLKP[:], T.QQ[:, CAP * b:CAP * b + CAP], True, True)],
+           "BLKP " + ("QW" if b == 3 else "QL%d" % b), "ps%d" % bank, CAP)
+    place_qt = {0: (1, 0), 3: (1, CAP), 1: (2, 0), 2: (2, CAP)}
+    for b in (3, 0, 1, 2):
+        now("s%d" % b)
+        spread(b)
+    now("qa")
+    move("S", T.QT[:, 0:2 * CAP], ps[1][:, :], "ps1", "QT", 2 * CAP)
+    now("o1")
+    sums(6, 0, WI_, T.QQ, 0, R4, True, True, "QL0 QL1 QL2 QW")
+    cp(T.O1[:], ps[6][:, 0:64], "ps6", "O1")
+    now("qb")
+    if 1 not in HELP1 or 1 not in HELP2:
+        move("S", T.QT[:, 2 * CAP:R3], ps[2][:, 0:CAP], "ps2", "QT1", CAP)
+    now("bits")
+    ts(T.WI[:], ps[4][:, 0:64], col(cSC), col(cBA), A.mult, A.add, "ps4 cSC cBA", "WI")
+    t1(T.WJ[:], T.WI[:], 1, A.bitwise_and, "WI", "WJ")
+    ts(T.PENA[:], T.WJ[:], -BIG, BIG, A.mult, A.add, "WJ", "PENA")
+    now("at")
+    move("S", T.G0[:], T.TS[:, :].indirect(T.RU[:, 0:4]), names("TS", nt) + " TSz RU", "G0", 100)
+    mm([(ps[5][:, 0:64], T.BLKP[:], T.G0[:], True, True)], "BLKP G0", "ps5")
+    move("S", T.LS[:, 208:401], ps[3][:, 0:193], "ps3", "SH", 193)
+    tt(T.PENU[:], ps[5][:, 0:64], T.PENA[:], A.add, "ps5 PENA", "PENU")
+    tt(T.AT[:], T.LS[:, 208:401].indirect(T.P2U[:, 0:4]), T.PENU[:], A.max, "SH P2U PENU", "AT", 160)
+    now("ib")
+    move("S", T.IB[:, 0:64], ps[6][:, 0:64], "ps6", "IB0", 64)
+    act(T.IB[:, 64:128], ps[6][:, 0:64], AF.Copy, "ps6", "IB1", 64, scale=16.0)
 
-    cp(T.O2[:, 48:64], ps[4][:, 0:16], "ps4", "O2o")
-    tt(T.CMQ[:, R3:R3 + CAP], T.P2[:, :].indirect(T.O2[:, 48:64]), T.QT[:, R3:R3 + CAP], A.is_le, "P2 O2o QT3", "CMQo")
-    sums(3, 0, W1, T.CMQ, R3, R3 + CAP, False, True, "CMQo")
-    t1(T.O3[:, 48:64], ps[3][:, 0:16], -1.0, A.add, "ps3", "O3o")
-    cp(T.AL[:, own:own + CAP], T.F[:, :].indirect(T.O3[:, 48:64]), "Fz F O3o", "ALo")
+    def carry():
+        now("head")
+        w = rank + 1
+        slot = lambda buf, s: buf[:, s:NI * w:w]
+        move("S", slot(T.CI, rank), XS(0, CB).indirect(T.RU[:, 0:4]), "RU XSz " + XSa, "CI%d" % rank, 100)
+        t1(slot(T.CZ, rank), slot(T.CI, rank), 0.0, A.is_equal, "CI%d CZz" % rank, "CZ%d" % rank)
+        now("carry")
+        for s in range(rank):
+            move("S", slot(T.CI, s), T.CT[:, s, :], "Lr", "CI%d" % s, 64)
+            if s > 0:
+                t1(slot(T.CZ, s), T.CT[:, s, :], 0.0, A.is_equal, "Lr CZz", "CZ%d" % s)
+        scan(T.CO[:, 0:NI * w], T.CZ[:, 0:NI * w], T.CI[:, 0:NI * w], 0.0, A.mult, A.add,
+             names("CZ", range(1, w)) + " " + names("CI", range(w)), "CO", 32 * w)
+        now("refill")
+        cp(XS(0, CB).indirect(T.RU[:, 0:4]), slot(T.CO, rank), "RU CO XSz", XSa, 60 + 64 * SCATTER)
+        scan(XS(FB, FB + M), T.Z[:, 0:M], XS(0, M), 0.0, A.mult, A.add, Za + " " + XSa, "F", M // 2)
+        now("spread")
+        move("S", XS(CB, CB + 1024), T.CO[:, 0:NI * w].indirect(T.UC[:, :]), "UC CO", "CR0 CR1", 1024 * GATHER)
 
-    for h in range(3):
-        move("S", T.AG[:, cs[h]], T.AL[:, :].indirect(T.POS[:, 16 * h:16 * h + 16]), "ALr ALo " + POS, "AG%d" % h)
-    for h in range(3):
-        bank = "ps%d" % h
-        t1(T.MZ[:, cs[h]], T.AG[:, cs[h]], 0.0, A.is_equal, "AG%d" % h, "MZ%d" % h)
-        tt(ps[h][:, 0:CAP], T.MZ[:, cs[h]], ps[h][:, 0:CAP], A.mult, "MZ%d %s" % (h, bank), bank)
-        tt(T.YB[:, cs[h]], T.AG[:, cs[h]], ps[h][:, 0:CAP], A.add, "AG%d %s" % (h, bank), "YB%d" % h)
-        dma("S" if h == 2 else "Y", T.y[:, cs[h]], T.YB[:, cs[h]], "YB%d" % h, "y%d" % h)
+    def level(out, table, off, blocks, helped, r, w):
+        for b in blocks:
+            cs, src, (bank, at) = slice(CAP * b, CAP * b + CAP), table[:, :].indirect(off[:, 16 * b:16 * b + 16]), place_qt[b]
+            if b not in helped:
+                at += 2 * CAP * (bank - 1)
+                tt(out[:, cs], src, T.QT[:, at:at + CAP], A.is_le, r + (" QT" if bank == 1 else " QT1"), "%s%d" % (w, b),
+                   60 + CAP * GATHER)
+            else:
+                move("S", T.GA[:, at:at + CAP], src, r, "GA%d" % b, CAP * GATHER)
+                tt(out[:, cs], T.GA[:, at:at + CAP], ps[2][:, at:at + CAP], A.is_le, "GA%d ps2" % b, "%s%d" % (w, b), CAP)
+
+    def seed(bank, at, j, a, b):
+        mm([(ps[bank][:, at:at + b - a], T.IDN[:, 0:128], T.IB[:, 64 * j + a:64 * j + b], True, False)], "IDN IB0 IB1", "ps%d" % bank)
+    now("l1")
+    level(T.CMP, T.AT, T.O1, (0, 3, 1, 2), HELP1, "AT O1", "CMP")
+    now("o2")
+    seed(6, 64, 0, 0, 64)
+    sums(6, 64, WA, T.CMP, 0, R4, False, True, names("CMP", range(4)))
+    cp(T.O2[:], ps[6][:, 64:128], "ps6", "O2")
+    now("p2")
+    move("S", T.LS[:, 0:192], ps[0][:, 0:192], "ps0", "L2", 192)
+    move("S", T.PG[:], T.LS[:, 0:208].indirect(T.P2U[:, 0:36]), "L2 L2z P2U", "PG", 576 * GATHER)
+    tt(T.P2[:, 0:512], T.PG[:, 0:512], ps[7][:, :], A.max, "PG ps7", "P2a", 512)
+    tt(T.P2[:, 512:576], T.PG[:, 512:576], ps[4][:, 64:128], A.max, "PG ps4", "P2b")
+    tt(T.P2[:, 0:64], T.P2[:, 0:64], ps[4][:, 128:192], A.min, "P2a ps4", "P2a")
+    Fw = lambda a: XS(CB, FB + M).indirect(T.O3[:, 16 * a:16 * a + 16])
+
+    def second(bank, blocks, k):
+        a, b = CAP * min(blocks), CAP * max(blocks) + CAP
+        now("wb" + k)
+        seed(bank, 0, 1, a // 16, b // 16)
+        sums(bank, 0, WB, T.CMP, a, b, False, False, names("CMP", blocks))
+        now("l2" + k)
+        level(T.CMQ, T.P2, T.O2, blocks, HELP2, "P2a P2b O2", "CMQ")
+        now("o3" + k)
+        sums(bank, 0, W1, T.CMQ, a, b, False, True, names("CMQ", blocks))
+        cp(T.O3[:, a // 16:b // 16], ps[bank][:, 0:(b - a) // 16], "ps%d" % bank, "O3" + k)
+    if rank > 0:
+        carry()
+    for bank, blocks, k in GROUPS:
+        second(bank, blocks, k)
+        now("ans" + k)
+        for a in blocks:
+            move(AENG[a], T.ANS[:, CAP * a:CAP * a + CAP], Fw(a), "CR0 CR1 CRb F O3" + k, "ANS%d" % a, CAP * GATHER)
+            me = send((rank - a - 1) % N, T.AL[:, CAP * (a + 1):CAP * (a + 2)], T.ANS[:, CAP * a:CAP * a + CAP], "ans",
+                      "ANS%d" % a, "_a")
+    landing("ALr", "ans", sum(len(topo.engines(T.cores[o], core)) for o in range(N) if o != rank), me, REMOTE)
+    second(4, (3,), "o")
+    now("end")
+    move("V", T.AL[:, 0:CAP], Fw(3), "CR0 CR1 CRb F O3o", "ALo", CAP * GATHER)
+
+    for h in range(4):
+        a, b = 192 * h, 192 * h + 192
+        move("SV"[h % 2], T.YB[:, a:b], T.AL[:, :].indirect(T.POS[:, a // 16:b // 16]), "ALr ALo POS", "YB%d" % h, 192 * GATHER)
+        if h % 2:
+            dma("Y", T.y[:, a - 192:b], T.YB[:, a - 192:b], "YB%d YB%d" % (h - 1, h), "y%d" % h)
+
+    for j, o in enumerate(ops):
+        o["j"] = j
+    gap = lambda d, hard: d["lag"] + (WAKE if hard else 0)
+    early = lambda o: GUARD if o["w"] in ("_q", "_a", "_l") else 0
+    pre = [[(d["j"], gap(d, True) - early(o)) for d in o["deps"]]
+           + [(d["j"], gap(d, False) if o["eng"] is None else 0) for d in o["after"]] for o in ops]
+    post = [[] for o in ops]
+    for j, es in enumerate(pre):
+        for i, w in es:
+            post[i].append((j, w))
+
+    def place(rank_of, before, tail):
+        end, busy, front = {}, {k: [] for k in queue}, {k: 0 for k in queue}
+        todo = sorted(range(len(ops)), key=rank_of)
+        while todo:
+            j = next(i for i in todo if all(d in end for d, w in before[i]))
+            todo.remove(j)
+            at, ns, eng = max([tail[j]] + [end[d] + w for d, w in before[j]]), ops[j]["ns"], ops[j]["eng"]
+            strict = eng in ("S", "P") or (eng == "V" and ns >= LONG)
+            if strict:
+                at = max(at, front[eng])
+            for a, b in busy.get(eng, []):
+                if at + ns <= a:
+                    break
+                at = max(at, b)
+            if strict:
+                front[eng] = at + ns
+            if ops[j]["eng"] is not None:
+                busy[ops[j]["eng"]] = sorted(busy[ops[j]["eng"]] + [(at, at + ns)])
+            end[j] = at + ns
+        return end
+    none, lags = [0] * len(ops), [o["lag"] for o in ops]
+    prio = [1000 * STEPS.index(o["step"]) + o["j"] for o in ops]
+    for j in reversed(range(nload, nconst)):
+        key = ops[j]["w"]
+        prio[j] = nload + EARLY.index(key) / 100 if key in EARLY else min(prio[i] for i, w in post[j]) - 0.5
+    end = place(lambda j: (prio[j], j), pre, none)
+    best = (max(end[j] + lags[j] for j in end), end)
+    for turn in range(ROUNDS):
+        back = place(lambda j: -end[j] - lags[j], post, lags)
+        end = place(lambda j: -back[j], pre, none)
+        span = max(end[j] + lags[j] for j in end)
+        if span < best[0]:
+            best = (span, end)
+    issue = [ops[j] for j in sorted(best[1], key=lambda j: (best[1][j] - ops[j]["ns"], j)) if ops[j]["eng"] is not None]
 
     count = {"V": 0, "S": 0, "P": 0, "G": 0}
-    for o in ops:
+    for o in issue:
         if o["dma"] is None and o["used"]:
             count[o["eng"]] += 1
             o["n"] = count[o["eng"]]
     waited = {}
-    for o in ops:
+    for o in issue:
         need = {}
         for d in o["deps"]:
             sem, val = d["ext"] if d["ext"] else ((d["dma"], 16) if d["dma"] else (d["eng"], d["n"]))
@@ -407,6 +549,6 @@ def rank_program(g, core, T, topo):
     for (eng, sem), val in waited.items():
         seen[sem] = max(seen.get(sem, 0), val)
     g.wait_ge(T.sem.sent, nsent[0])
-    for o in ops:
+    for o in issue:
         if o["dma"] and seen.get(o["dma"], 0) < 16:
             queue[o["eng"]].wait_ge(T.sem[o["dma"]], 16)

from concourse.bass import DstId, RemoteDMATransfer
from concourse.mybir import AluOpType as A, AxisListType, ActivationFunctionType as AF

M, NI, Q, CAP = 3072, 64, 768, 256
BIG = float(2 ** 23)
RND = 1.5 * 2.0 ** 43
CB = M + 96
FB = CB + 16 * NI + 1
DUMP = M + 16
R7, R14 = 1.5 * 2.0 ** 30, 1.5 * 2.0 ** 37
EARLY = ("ONE TWz0 IP0 TMPA IO TRI I4 BLK TRC I12 TWO GRa L2z TWz2 FL0 FL1 FL2 FL3 QRz IP1 cK D QW DK TWz1 BIGT WSz IDN WS0 "
         "BLKP TSz Zz").split()
HELP1 = (2,)
HELP2 = (2,)
XCUT = (0, 1280, 2048, M)
XENG = "SSV"
TCUT = (0, 1024, 2048, M)
TENG = "SSS"
STEPS = ("load tpieces qpieces slot pmu power scales bounds scatter cols x0 lists t0 x2 z0 x1 z1 z2 fill s3 f0 u0 bits t1 t2 "
         "f1 u1 s0 f2 at qa o1 weights s1 s2 head ib qb u2 l1 o2 carry p2 wba l2a refill spread o3a wbo ansa l2o o3o end").split()
LAST = 11000
GATHER, SCATTER = 1.56, 3.8
CYC = 0.85
WAKE = 100
LOCAL = 1000
REMOTE = 2200
ROUNDS = 0
GROUPS = ((7, (0, 1, 2), "a"),)
AENG = "VSS"
LONG = 400
GUARD = 0
F32, BF, I32, U16 = "float32", "bfloat16", "int32", "uint16"
_S = {
    BF: dict(X=M, BUF=CB + 1024 + CB, Z=CB, TW=M, TS=M + 144, TP=[4, 240], QR=Q, QQ=7 * CAP, E=[4, 50], ONE=128,
             TMPA=128, BLK=[8, 16], TRI=128, TRC=128, BLKP=[8, 16], B3=[3, 8, 16], IDN=128, WS=576, OH=192, XE=192,
             G0=64, CMP=4 * CAP, CMQ=4 * CAP, ANS=3 * CAP, AL=4 * CAP, CT=[3, 64], CI=256, CZ=256, CO=256,
             IB=128, YB=Q, IO=192, BIGT=64, S16=4, CW=8),
    F32: dict(QXF=64, QF=48, QS=48, FL=192, CN=192, CN3=96, PC=48, QT=3 * CAP, GA=2 * CAP, KC=24, GR=16, TWO=8,
              GT=16, D=12, I4=4, SM=32, PENA=64, PENU=64, LS=408, AT=64, PG=576, P2=576),
    I32: dict(PM=192, TB=240, QI=96, QX=[2, 2, 16], IP=8, I12=12, SE=8, XT=16, WI=64, WJ=64, IC=64),
    U16: dict(PMU=192, POS=48, U12=12, P2U=36, RU=8, O1=64, O2=64, O3=64, UC=64),
}
SCRATCH = {_n: ("sbuf", [128] + (_c if isinstance(_c, list) else [_c]), _d) for _d in _S for _n, _c in _S[_d].items()}
for _b in range(8):
    SCRATCH["ps%d" % _b] = ("psum", [128, 512], F32)

SEMAPHORES = ["V", "S", "P", "G", "sent", "q0", "q1", "q2", "ans", "last"] + ["d%d" % _i for _i in range(32)]


def rank_program(g, core, T, topo):
    rank = T.rank_of(core)
    if rank is None:
        return
    N = len(T.cores)
    queue = {"V": g.vector, "S": g.scalar, "P": g.tensor, "G": g, "Y": g.sync}
    V, S, P = g.vector, g.scalar, g.tensor
    ops, state, ndma, nsent, step = [], {}, [0], [0], ["load"]

    def now(name):
        step[0] = name

    def op(eng, fn, r, w, ns, lag=0, dma=False):
        me = {"eng": eng, "fn": fn, "deps": [], "after": [], "dma": None, "used": False, "ext": None, "ns": ns, "lag": lag,
              "w": w, "step": step[0]}
        if dma:
            me["dma"] = "d%d" % ndma[0]
            ndma[0] += 1
        for k in r.split():
            st = state[k]
            me["deps"].append(st["w"])
            if k.startswith("ps"):
                me["deps"] += [o for o in st["r"] if o["eng"] != eng]
        for k in w.split():
            st = state.setdefault(k, {"w": None, "r": []})
            for o in ([st["w"]] if st["w"] is not None else []) + st["r"]:
                me["after" if k[0] == "_" or eng == o["eng"] == "P" else "deps"].append(o)
        for k in r.split():
            state[k]["r"].append(me)
        for k in w.split():
            state[k] = {"w": me, "r": []}
        for o in me["deps"]:
            o["used"] = True
        ops.append(me)
        return me

    def landing(key, sem, val, like, lag):
        me = {"eng": None, "dma": None, "ext": (sem, val), "used": True, "deps": [], "after": [like], "ns": 0, "lag": lag,
              "step": step[0]}
        ops.append(me)
        state[key] = {"w": me, "r": []}

    def vec(fn, r, w, n):
        return op("V", fn, r, w, max(n, 64) * CYC)

    def ts(out, in0, s1, s2, op0, op1, r, w, n=64):
        vec(lambda: V.tensor_scalar(out, in0, s1, s2, op0, op1), r, w, n)

    def t1(out, in0, s1, op0, r, w, n=64):
        vec(lambda: V.tensor_scalar(out, in0, s1, None, op0), r, w, n)

    def tt(out, in0, in1, o, r, w, n=64):
        vec(lambda: V.tensor_tensor(out, in0, in1, o), r, w, n)

    def cp(out, in_, r, w, n=64):
        return vec(lambda: V.tensor_copy(out, in_), r, w, n)

    def ms(ap, c, w, n=64):
        vec(lambda: V.memset(ap, c), "", w, n)

    def scan(out, d0, d1, init, op0, op1, r, w, n=64):
        return vec(lambda: V.tensor_tensor_scan(out, d0, d1, init, op0, op1), r, w, n)

    def act(out, in_, f, r, w, n=8, **kw):
        op("S", lambda: S.activation(out, in_, f, **kw), r, w, 65 + n * CYC)

    def lin(out, in_, scale, bias, r, w):
        act(out, in_, AF.Identity, r, w, scale=scale, bias=bias)

    def move(eng, out, in_, r, w, n):
        if eng == "S":
            act(out, in_, AF.Copy, r, w, n)
        else:
            cp(out, in_, r, w, n + 60)

    def mm(items, r, w, n=64):
        def fn():
            last = None
            for (o, l, rh, st, sp) in items:
                last = P.matmul(o, l, rh, st, sp)
            return last
        op("P", fn, r, w, len(items) * max(n, 64) * CYC)

    def dma(eng, out, in_, r, w, lag=LOCAL):
        op(eng, lambda: queue[eng].dma_start(out, in_), r, w + " _" + eng, 60, lag, True)

    def iota(out, pattern, base, cm, w, n, flag=True):
        if flag:
            op("G", lambda: g.iota(out, pattern, base, cm, allow_small_or_imprecise_dtypes=True), "", w, 130 + 2 * n * CYC)
        else:
            op("G", lambda: g.iota(out, pattern, base, cm), "", w, 130 + 2 * n * CYC)

    def zero(out, w, n):
        iota(out, [[0, n]], 0, 0, w, n)

    def sel(out, in_, pattern, cmp, base, cm, r, w, n=128):
        op("G", lambda: g.affine_select(out, in_, pattern, cmp, 0.0, base, cm), r, w, 170 + 2 * n * CYC)

    def send(dst_rank, out, in_, sem, r, w):
        dst = T.cores[dst_rank]
        rid, pid = topo.addr(dst, core)
        mask = topo.mask(core, dst)
        nsent[0] += len(topo.engines(core, dst))
        return op("G", lambda: g.remote_dma(out, in_, T.sem[sem], T.sem.sent, pid, rid, mask), r, w, 500)

    def shared(src):
        sets = [topo.engines(T.cores[src], T.cores[o]) for o in range(src + 1, N)]
        return [e for e in sets[0] if all(e in s for s in sets)]

    ps = [T["ps%d" % b] for b in range(8)]
    KC = T.KC
    col = lambda j: KC[:, j:j + 1]
    cK, cWB, cPW, cSC, cBA, cNK, cM7, cT1, cT2, cK1, cWA = range(11)

    def slide(x, m):
        return T.WS[:, 144 * x + 15 - m:144 * x + 143 - m]
    W1, WI_, WA, WB = range(4)
    wcol = lambda x: T.WS[:, 144 * x + 15:144 * x + 143:16]

    def sums(b, c0, x, src, lo, hi, start, stop, r):
        out = ps[b][:, c0:c0 + (hi - lo) // 16]
        mm([(out, slide(x, m), src[:, lo + m:hi:16], start and m == 0, stop and m == 15) for m in range(16)],
           "WS%d %s" % (x, r), "ps%d" % b, (hi - lo) // 16)

    R3, R4 = 3 * CAP, 4 * CAP
    QW = lambda a, b: T.QQ[:, R3 + a:R3 + b]
    XS = lambda a, b: T.BUF[:, a:b]
    names = lambda k, js: " ".join("%s%d" % (k, j) for j in js)

    for b in range(2):
        for h in range(2):
            dma("YS"[h], T.QX[:, b, h, :], T.qt[h:8:2, 256 * b:256 * b + 512], "", "QX%d%d" % (b, h), LOCAL + 400)
    dma("Y", T.TB[:, 192:240], T.qt[:], "", "QB", LOCAL + 700)
    dma("S", T.QI[:, 0:48], T.qi[:], "", "QI", LOCAL + 800)
    dma("S", T.TB[:, 0:192], T.times[:], "", "TB", LOCAL + 1100)
    dma("Y", T.PM[:], T.pm[:], "", "PM", LOCAL + 1300)
    dma("S", T.SE[:, 0:4], T.starts[:, 0:64], "", "SEs", LOCAL + 1500)
    dma("Y", T.SE[:, 4:8], T.starts[:, 1:65], "", "SEe", LOCAL + 1600)
    dma("Y", T.X[:], T.x[:], "", "X", LOCAL + 3200)

    nload = len(ops)
    ms(T.ONE[:], 1.0, "ONE")
    ms(T.TW[:, 0:1024], 0.0, "TWz0", 512)
    ms(T.E[:, :, 1], 0.0, "Ez")
    move("S", T.QR[:], T.TW[:, 0:Q], "TWz0", "QRz", Q)
    move("S", QW(0, R4), T.TW[:, 0:R4], "TWz0", "QW", R4)
    move("S", T.TW[:, 1024:2048], T.TW[:, 0:1024], "TWz0", "TWz1", 1024)
    zero(T.TW[:, 2048:M], "TWz2", 1024)
    iota(T.TWO[:], [[0, 8]], 2, 0, "TWO", 8)
    iota(T.GR[:, 0:8], [[0, 8]], 256, 0, "GRa", 8)
    zero(T.LS[:, 192:208], "L2z", 16)
    iota(T.IP[:, 0:1], [[0, 1]], 0, 1, "IP0", 1, False)
    iota(T.I4[:], [[16, 4]], DUMP, 0, "I4", 4)
    for b in range(N):
        act(T.FL[:, 48 * b:48 * b + 48], T.ONE[:, 0:48], AF.Copy, "ONE", "FL%d" % b, 48, scale=CAP * b - 1.0)
    iota(T.IO[:], [[0, 12], [1, 16]], 0, 0, "IO", 192)
    iota(T.I12[:], [[1, 12]], 0, 0, "I12", 12, False)
    act(T.BIGT[:], T.ONE[:, 0:64], AF.Copy, "ONE", "BIGT", 64, scale=BIG)
    grp, neg, lo8, hi8 = [[-16, 8], [0, 16]], [[16, 8], [0, 16]], [[0, 8], [-1, 16]], [[0, 8], [1, 16]]
    sel(T.TMPA[:], T.ONE[:, 0:128], grp, A.is_ge, 0, 1, "ONE", "TMPA")
    sel(T.BLK[:], T.TMPA[:], neg, A.is_ge, 15, -1, "TMPA", "BLK")
    sel(T.TRI[:], T.TMPA[:], [[1, 128]], A.is_ge, 0, -1, "TMPA", "TRI")
    sel(T.TRC[:], T.BLK[:], [[-1, 128]], A.is_gt, 0, 1, "BLK", "TRC")
    sel(T.BLKP[:], T.TMPA[:], neg, A.is_ge, 2, -1, "TMPA", "BLKP")
    sel(T.B3[:, 0], T.BLK[:], lo8, A.is_ge, 7, 0, "BLK", "B30")
    sel(T.B3[:, 1], T.BLK[:], hi8, A.is_ge, -8, 0, "BLK", "B31")
    sel(T.IDN[:], T.ONE[:], [[-1, 128]], A.is_equal, 0, 1, "ONE", "IDN")
    zero(T.WS[:], "WSz", 576)
    iota(T.CW[:], [[0, 8]], 16, 0, "CW", 8)
    sel(wcol(WI_), T.CW[:], [[-16, 8]], A.is_equal, -3, 1, "CW WSz", "WS1", 8)
    sel(wcol(W1), T.TMPA[:, 0:128:16], [[16, 8]], A.is_ge, 15, -1, "TMPA WSz", "WS0", 8)
    zero(T.TS[:, M:M + 144], "TSz", 144)
    zero(T.Z[:, M:CB], "Zz", 96)
    if rank < N - 1:
        zero(XS(FB + M, FB + M + 95), "Fz", 95)
    zero(XS(CB + 1024, FB), "CRb", 1)
    if rank == 0:
        for h in range(2):
            zero(XS(CB + 512 * h, CB + 512 * h + 512), "CR%d" % h, 512)
    else:
        iota(T.IC[:], [[rank + 1, 64]], rank - 1, 0, "IC", 64, False)
        cp(T.UC[:], T.IC[:], "IC", "UC")
        zero(XS(M, CB), "XSz", 96)
        zero(T.CZ[:, 0:NI * (rank + 1):rank + 1], "CZz", 64)
    t1(T.IP[:, 4:5], T.IP[:, 0:1], 15, A.bitwise_and, "IP0", "IP1")
    scan(T.GR[:, 8:16], T.TWO[:], T.LS[:, 192:200], 8.0, A.mult, A.add, "TWO L2z", "GRb")
    cp(KC[:, 0:1], T.IP[:, 4:5], "IP1", "cK")
    cp(T.U12[:], T.I12[:], "I12", "U12")
    ts(T.OH[:], T.IO[:], col(cK), -BIG, A.is_equal, A.mult, "IO cK", "OH", 96)
    lin(T.D[:, 0:4], T.I4[:], 1.0, col(cK), "I4 cK", "D")
    lin(T.D[:, 8:12], T.D[:, 0:4], -16.0, 16.0 * (DUMP + NI), "D", "DK")
    nconst = len(ops)
    now("power")
    t1(col(cM7), col(cK), 7.0, A.is_le, "cK", "cM7")
    tt(T.GT[:], T.GR[:], T.OH[:, 0:16], A.mult, "GRa GRb OH", "GT")
    vec(lambda: V.tensor_reduce(col(cPW), T.GT[:], AxisListType.X, A.add), "GT", "cPW", 64)
    vec(lambda: V.reciprocal(col(cSC), col(cPW)), "cPW", "cSC", 220)
    now("scales")
    lin(col(cT1), col(cK), -1.0 / 16, 239.0 / 256, "cK", "cT1")
    lin(col(cBA), col(cT1), col(cM7), -0.5 + 1.0 / 512, "cT1 cM7", "cBA")
    lin(col(cT2), col(cM7), -240.0, 0.0, "cM7", "cT2")
    lin(col(cWA), col(cM7), 64.0, 0.0, "cM7", "cWA")
    now("weights")
    lin(col(cWB), col(cPW), -1.0 / BIG, col(cT2), "cPW cT2", "cWB")
    act(wcol(WA), T.BLK[:, :, 0], AF.Copy, "BLK WSz cWA", "WS2", scale=col(cWA))
    act(wcol(WB), T.BLK[:, :, 0], AF.Copy, "BLK WSz cWB", "WS3", scale=col(cWB))

    now("slot")
    ts(T.QXF[:], T.QX[:], 0.5 - 2.0 ** 19, RND, A.add, A.add, "QX00 QX01 QX10 QX11", "QXF")
    vec(lambda: V.transpose(T.QS[:, 16:48], T.QXF[:, 32:64]), "QXF", "QS", 64)
    vec(lambda: V.transpose(T.QS[:, 0:32], T.QXF[:, 0:32]), "QXF", "QS", 64)
    for b in range(N):
        t1(T.E[:, b, 2:50], T.QS[:], RND + 2.0 ** 20 * ((rank + b) % N), A.is_equal, "QS Ez", "E%d" % b)
    Es = names("E", range(N))
    mm([(ps[0][:, 0:192], T.TRI[:], T.E[:, :, 2:50], True, False),
        (ps[0][:, 0:192], T.TRC[:], T.E[:, :, 1:49], False, True)], "TRI TRC " + Es, "ps0", 192)
    def pieces(bank, a, b, r, w):
        mid, key = ps[bank][:, 0:b - a], "ps%d" % bank
        ts(T.TP[:, 0, a:b], T.TB[:, a:b], R14, R14, A.add, A.subtract, r, w + "0", b - a)
        ts(mid, T.TB[:, a:b], R7, R7, A.add, A.subtract, r, key, b - a)
        tt(T.TP[:, 1, a:b], mid, T.TP[:, 0, a:b], A.subtract, "%s %s0" % (key, w), w + "1", b - a)
        tt(T.TP[:, 2, a:b], T.TB[:, a:b], mid, A.subtract, "%s %s" % (key, r), w + "2", b - a)
    now("qpieces")
    pieces(3, 192, 240, "QB", "QP")
    t1(T.QI[:, 48:96], T.QI[:, 0:48], 2, A.arith_shift_right, "QI", "QH")
    t1(T.QF[:], T.QI[:, 48:96], -63.0 / 16, A.mult, "QH", "QF")
    tt(T.TP[:, 3, 192:240], T.QI[:, 0:48], T.QF[:], A.add, "QI QF", "QP3", 96)
    for j in range(4):
        dma("Y", T.QR[j:128:16, :], T.TP[:, j, 192:240], "QP%d QRz" % j, "QR%d" % j, LOCAL + 1200)
    now("pmu")
    cp(T.PMU[:], T.PM[:], "PM", "PMU", 192)
    now("tpieces")
    pieces(2, 0, 192, "TB", "TP")
    for j in range(3):
        dma("Y", T.TW[j:128:16, :], T.TP[:, j, 0:192], "TP%d TWz0 TWz1 TWz2" % j, "TW%d" % j, LOCAL + 200)
    now("slot")
    scan(ps[1][:, 0:192], T.FL[:], ps[0][:, 0:192], -1.0, A.max, A.add, names("FL", range(N)) + " ps0", "ps1", 192)
    tt(T.CN[:], ps[1][:, 0:192], T.E[:, :, 2:50], A.mult, "ps1 " + Es, "CN", 192)
    tt(T.CN3[:], T.CN[:, 0:96], T.CN[:, 96:192], A.add, "CN", "CN3", 192)
    tt(T.PC[:], T.CN3[:, 0:48], T.CN3[:, 48:96], A.add, "CN3", "PC", 96)
    cp(T.POS[:], T.PC[:], "PC", "POS")

    now("scatter")
    cp(QW(0, R4).indirect(T.POS[:, :]), T.QR[:], "POS QR0 QR1 QR2 QR3", "QW", Q * SCATTER)
    for b in range(1, N):
        me = send((rank + b) % N, T.QQ[:, CAP * (b - 1):CAP * b], QW(CAP * b, CAP * b + CAP), "q%d" % (b - 1), "QW", "_q")
        landing("QL%d" % (b - 1), "q%d" % (b - 1), len(topo.engines(T.cores[(rank - b) % N], core)), me, REMOTE + 600 + 250 * b)

    s_, e_ = T.SE[:, 0:4], T.SE[:, 4:8]
    r_ = T.XT[:, 4:8]
    ln, big, dm, vv, ru, lu = [T.SM[:, 4 * j:4 * j + 4] for j in range(6)]
    SEs, SEe = "SEs", "SEe"
    now("bounds")
    tt(ln, e_, s_, A.subtract, SEs + " " + SEe, "ln")
    t1(r_, s_, 15, A.bitwise_and, SEs, "r")
    t1(big, ln, 4096.0, A.mult, "ln", "big")
    tt(T.S16[:], s_, r_, A.subtract, SEs + " r", "S16")
    tt(T.XT[:, 0:4], ln, r_, A.add, "ln r", "XT0")
    tt(vv, T.S16[:], T.D[:, 8:12], A.add, "S16 DK", "vv")
    tt(T.XT[:, 8:12], vv, big, A.min, "vv big", "XT2")
    tt(T.XE[:], T.XT[:, 0:12].indirect(T.U12[:, 0:12]), T.OH[:], A.mult, "XT0 r XT2 U12 OH", "XE", 360)

    def plus16(out, n, src):
        return [(out, T.ONE[0:16 * n, :], src[0:16 * n, :], False, False)] if n else []

    def bound(out, xe, n):
        return [(out, T.BLK[:], xe, True, False)] + plus16(out, n, T.BIGT) + [(out, T.TRI[:], T.BIGT[:], False, True)]
    mm(sum([bound(ps[7][:, 64 * n:64 * n + 64], T.XE[:, 0:64], n) for n in range(8)], []), "BLK TRI ONE BIGT XE", "ps7")
    mm(bound(ps[4][:, 64:128], T.XE[:, 0:64], 8) + bound(ps[4][:, 128:192], T.XE[:, 64:128], 0), "BLK TRI ONE BIGT XE", "ps4")
    now("bits")
    mm([(ps[4][:, 0:64], T.B3[:, 0], T.XE[:, 0:64], True, False),
        (ps[4][:, 0:64], T.B3[:, 1], T.XE[:, 128:192], False, True)], "B30 B31 XE", "ps4")

    now("cols")
    mm([(ps[5][:, 0:4], T.IDN[:], T.S16[:], True, True)]
       + sum([[(ps[5][:, 4 * n:4 * n + 4], T.IDN[:], T.S16[:], True, False),
               (ps[5][:, 4 * n:4 * n + 4], T.ONE[0:16 * n, :], T.ONE[0:16 * n, 0:4], False, True)] for n in range(1, 9)], []),
       "ONE IDN S16", "ps5")
    t1(T.P2U[:], ps[5][:, 0:36], 1.0 / 16, A.mult, "ps5", "P2U")
    now("lists")
    tt(dm, T.D[:, 0:4], big, A.subtract, "D big", "dm")
    tt(ru, s_, dm, A.max, SEs + " dm", "ru")
    tt(lu, e_, dm, A.max, SEe + " dm", "lu")
    cp(T.RU[:], T.SM[:, 16:24], "ru lu", "RU")

    def order(eng, dst, src, a, b, r, w):
        move(eng, dst[:, a:b], src[:, :].indirect(T.PMU[:, a // 16:b // 16]), "PMU " + r, w, (b - a) * GATHER)
    nx, nt = range(len(XCUT) - 1), range(len(TCUT) - 1)
    scut = [0] + [c // 16 - 8 for c in TCUT[1:-1]] + [193]

    def firsts(h):
        a, b = scut[h], scut[h + 1]
        now("f%d" % h)
        mm([(ps[3][:, a:b], slide(W1, k), T.TS[:, 16 * (a + k + 1):16 * (b + k) + 1:16], k == 0, k == 7)
            for k in range(8)], "WS0 TSz " + names("TS", range(max(h - 1, 0), h + 1)), "ps3", b - a)

    def turn(h):
        now("u%d" % h)
        sums(0, TCUT[h] // 16, W1, T.TS, TCUT[h], TCUT[h + 1], True, True, "TS%d" % h)

    for h in nx:
        a, b = XCUT[h], XCUT[h + 1]
        now("x%d" % h)
        order(XENG[h], T.BUF, T.X, a, b, "X", "XS%d" % h)
        now("z%d" % h)
        t1(T.Z[:, a:b], XS(a, b), 0.0, A.is_equal, "XS%d" % h, "Z%d" % h, (b - a) // 2)
    for h in nt:
        now("t%d" % h)
        order(TENG[h], T.TS, T.TW, TCUT[h], TCUT[h + 1], "TW0 TW1 TW2", "TS%d" % h)
        firsts(h)
        turn(h)
    XSa, Za = names("XS", nx), names("Z", nx)
    now("fill")
    me = cp(T.Z[:, :].indirect(T.RU[:, 0:4]), T.TS[:, M:M + 64], "RU TSz Zz", Za, 60 + 64 * SCATTER)
    landing("Lr", "last", sum(len(shared(o)) for o in range(rank)), me, M // 2 * CYC + REMOTE + 900)
    if rank < N - 1:
        scan(XS(FB, FB + M), T.Z[:, 0:M], XS(0, M), 0.0, A.mult, A.add, Za + " " + XSa, "F", M // 2)
        mine = T.CT[:, rank, :]
        move("V", mine, XS(FB - 1, FB + M + 95).indirect(T.RU[:, 4:8]), "CRb Fz F RU", "Lo", 100)
        ids = [topo.addr(T.cores[o], core) for o in range(rank + 1, N)]
        nsent[0] += len(shared(rank))
        op("G", lambda: g.remote_dma_fused(
            [RemoteDMATransfer(dst_ids=[DstId(rid=a[0], pnc=a[1]) for a in ids], dma_engine_mask=sum(1 << e for e in shared(rank)),
                               remote_sem=T.sem["last"], srcs=[mine], dsts=[mine for a in ids])], local_sem=T.sem.sent),
           "Lo", "_l", 500, LAST)

    def spread(b):
        bank, at = place_qt[b]
        mm([(ps[bank][:, at:at + CAP], T.BLKP[:], T.QQ[:, CAP * b:CAP * b + CAP], True, True)],
           "BLKP " + ("QW" if b == 3 else "QL%d" % b), "ps%d" % bank, CAP)
    place_qt = {0: (1, 0), 3: (1, CAP), 1: (2, 0), 2: (2, CAP)}
    for b in (3, 0, 1, 2):
        now("s%d" % b)
        spread(b)
    now("qa")
    move("S", T.QT[:, 0:2 * CAP], ps[1][:, :], "ps1", "QT", 2 * CAP)
    now("o1")
    sums(6, 0, WI_, T.QQ, 0, R4, True, True, "QL0 QL1 QL2 QW")
    cp(T.O1[:], ps[6][:, 0:64], "ps6", "O1")
    now("qb")
    if 1 not in HELP1 or 1 not in HELP2:
        move("S", T.QT[:, 2 * CAP:R3], ps[2][:, 0:CAP], "ps2", "QT1", CAP)
    now("bits")
    ts(T.WI[:], ps[4][:, 0:64], col(cSC), col(cBA), A.mult, A.add, "ps4 cSC cBA", "WI")
    t1(T.WJ[:], T.WI[:], 1, A.bitwise_and, "WI", "WJ")
    ts(T.PENA[:], T.WJ[:], -BIG, BIG, A.mult, A.add, "WJ", "PENA")
    now("at")
    move("S", T.G0[:], T.TS[:, :].indirect(T.RU[:, 0:4]), names("TS", nt) + " TSz RU", "G0", 100)
    mm([(ps[5][:, 0:64], T.BLKP[:], T.G0[:], True, True)], "BLKP G0", "ps5")
    move("S", T.LS[:, 208:401], ps[3][:, 0:193], "ps3", "SH", 193)
    tt(T.PENU[:], ps[5][:, 0:64], T.PENA[:], A.add, "ps5 PENA", "PENU")
    tt(T.AT[:], T.LS[:, 208:401].indirect(T.P2U[:, 0:4]), T.PENU[:], A.max, "SH P2U PENU", "AT", 160)
    now("ib")
    move("S", T.IB[:, 0:64], ps[6][:, 0:64], "ps6", "IB0", 64)
    act(T.IB[:, 64:128], ps[6][:, 0:64], AF.Copy, "ps6", "IB1", 64, scale=16.0)

    def carry():
        now("head")
        w = rank + 1
        slot = lambda buf, s: buf[:, s:NI * w:w]
        move("S", slot(T.CI, rank), XS(0, CB).indirect(T.RU[:, 0:4]), "RU XSz " + XSa, "CI%d" % rank, 100)
        t1(slot(T.CZ, rank), slot(T.CI, rank), 0.0, A.is_equal, "CI%d CZz" % rank, "CZ%d" % rank)
        now("carry")
        for s in range(rank):
            move("S", slot(T.CI, s), T.CT[:, s, :], "Lr", "CI%d" % s, 64)
            if s > 0:
                t1(slot(T.CZ, s), T.CT[:, s, :], 0.0, A.is_equal, "Lr CZz", "CZ%d" % s)
        scan(T.CO[:, 0:NI * w], T.CZ[:, 0:NI * w], T.CI[:, 0:NI * w], 0.0, A.mult, A.add,
             names("CZ", range(1, w)) + " " + names("CI", range(w)), "CO", 32 * w)
        now("refill")
        cp(XS(0, CB).indirect(T.RU[:, 0:4]), slot(T.CO, rank), "RU CO XSz", XSa, 60 + 64 * SCATTER)
        scan(XS(FB, FB + M), T.Z[:, 0:M], XS(0, M), 0.0, A.mult, A.add, Za + " " + XSa, "F", M // 2)
        now("spread")
        move("S", XS(CB, CB + 1024), T.CO[:, 0:NI * w].indirect(T.UC[:, :]), "UC CO", "CR0 CR1", 1024 * GATHER)

    def level(out, table, off, blocks, helped, r, w):
        for b in blocks:
            cs, src, (bank, at) = slice(CAP * b, CAP * b + CAP), table[:, :].indirect(off[:, 16 * b:16 * b + 16]), place_qt[b]
            if b not in helped:
                at += 2 * CAP * (bank - 1)
                tt(out[:, cs], src, T.QT[:, at:at + CAP], A.is_le, r + (" QT" if bank == 1 else " QT1"), "%s%d" % (w, b),
                   60 + CAP * GATHER)
            else:
                move("S", T.GA[:, at:at + CAP], src, r, "GA%d" % b, CAP * GATHER)
                tt(out[:, cs], T.GA[:, at:at + CAP], ps[2][:, at:at + CAP], A.is_le, "GA%d ps2" % b, "%s%d" % (w, b), CAP)

    def seed(bank, at, j, a, b):
        mm([(ps[bank][:, at:at + b - a], T.IDN[:, 0:128], T.IB[:, 64 * j + a:64 * j + b], True, False)], "IDN IB0 IB1", "ps%d" % bank)
    now("l1")
    level(T.CMP, T.AT, T.O1, (0, 3, 1, 2), HELP1, "AT O1", "CMP")
    now("o2")
    seed(6, 64, 0, 0, 64)
    sums(6, 64, WA, T.CMP, 0, R4, False, True, names("CMP", range(4)))
    cp(T.O2[:], ps[6][:, 64:128], "ps6", "O2")
    now("p2")
    move("S", T.LS[:, 0:192], ps[0][:, 0:192], "ps0", "L2", 192)
    move("S", T.PG[:], T.LS[:, 0:208].indirect(T.P2U[:, 0:36]), "L2 L2z P2U", "PG", 576 * GATHER)
    tt(T.P2[:, 0:512], T.PG[:, 0:512], ps[7][:, :], A.max, "PG ps7", "P2a", 512)
    tt(T.P2[:, 512:576], T.PG[:, 512:576], ps[4][:, 64:128], A.max, "PG ps4", "P2b")
    tt(T.P2[:, 0:64], T.P2[:, 0:64], ps[4][:, 128:192], A.min, "P2a ps4", "P2a")
    Fw = lambda a: XS(CB, FB + M).indirect(T.O3[:, 16 * a:16 * a + 16])

    def second(bank, blocks, k):
        a, b = CAP * min(blocks), CAP * max(blocks) + CAP
        now("wb" + k)
        seed(bank, 0, 1, a // 16, b // 16)
        sums(bank, 0, WB, T.CMP, a, b, False, False, names("CMP", blocks))
        now("l2" + k)
        level(T.CMQ, T.P2, T.O2, blocks, HELP2, "P2a P2b O2", "CMQ")
        now("o3" + k)
        sums(bank, 0, W1, T.CMQ, a, b, False, True, names("CMQ", blocks))
        cp(T.O3[:, a // 16:b // 16], ps[bank][:, 0:(b - a) // 16], "ps%d" % bank, "O3" + k)
    if rank > 0:
        carry()
    for bank, blocks, k in GROUPS:
        second(bank, blocks, k)
        now("ans" + k)
        for a in blocks:
            move(AENG[a], T.ANS[:, CAP * a:CAP * a + CAP], Fw(a), "CR0 CR1 CRb F O3" + k, "ANS%d" % a, CAP * GATHER)
            me = send((rank - a - 1) % N, T.AL[:, CAP * (a + 1):CAP * (a + 2)], T.ANS[:, CAP * a:CAP * a + CAP], "ans",
                      "ANS%d" % a, "_a")
    landing("ALr", "ans", sum(len(topo.engines(T.cores[o], core)) for o in range(N) if o != rank), me, REMOTE)
    second(4, (3,), "o")
    now("end")
    move("V", T.AL[:, 0:CAP], Fw(3), "CR0 CR1 CRb F O3o", "ALo", CAP * GATHER)

    for h in range(4):
        a, b = 192 * h, 192 * h + 192
        move("SV"[h % 2], T.YB[:, a:b], T.AL[:, :].indirect(T.POS[:, a // 16:b // 16]), "ALr ALo POS", "YB%d" % h, 192 * GATHER)
        if h % 2:
            dma("Y", T.y[:, a - 192:b], T.YB[:, a - 192:b], "YB%d YB%d" % (h - 1, h), "y%d" % h)

    for j, o in enumerate(ops):
        o["j"] = j
    gap = lambda d, hard: d["lag"] + (WAKE if hard else 0)
    early = lambda o: GUARD if o["w"] in ("_q", "_a", "_l") else 0
    pre = [[(d["j"], gap(d, True) - early(o)) for d in o["deps"]]
           + [(d["j"], gap(d, False) if o["eng"] is None else 0) for d in o["after"]] for o in ops]
    post = [[] for o in ops]
    for j, es in enumerate(pre):
        for i, w in es:
            post[i].append((j, w))

    def place(rank_of, before, tail):
        end, busy, front = {}, {k: [] for k in queue}, {k: 0 for k in queue}
        todo = sorted(range(len(ops)), key=rank_of)
        while todo:
            j = next(i for i in todo if all(d in end for d, w in before[i]))
            todo.remove(j)
            at, ns, eng = max([tail[j]] + [end[d] + w for d, w in before[j]]), ops[j]["ns"], ops[j]["eng"]
            strict = eng in ("S", "P") or (eng == "V" and ns >= LONG)
            if strict:
                at = max(at, front[eng])
            for a, b in busy.get(eng, []):
                if at + ns <= a:
                    break
                at = max(at, b)
            if strict:
                front[eng] = at + ns
            if ops[j]["eng"] is not None:
                busy[ops[j]["eng"]] = sorted(busy[ops[j]["eng"]] + [(at, at + ns)])
            end[j] = at + ns
        return end
    none, lags = [0] * len(ops), [o["lag"] for o in ops]
    prio = [1000 * STEPS.index(o["step"]) + o["j"] for o in ops]
    for j in reversed(range(nload, nconst)):
        key = ops[j]["w"]
        prio[j] = nload + EARLY.index(key) / 100 if key in EARLY else min(prio[i] for i, w in post[j]) - 0.5
    end = place(lambda j: (prio[j], j), pre, none)
    best = (max(end[j] + lags[j] for j in end), end)
    for turn in range(ROUNDS):
        back = place(lambda j: -end[j] - lags[j], post, lags)
        end = place(lambda j: -back[j], pre, none)
        span = max(end[j] + lags[j] for j in end)
        if span < best[0]:
            best = (span, end)
    issue = [ops[j] for j in sorted(best[1], key=lambda j: (best[1][j] - ops[j]["ns"], j)) if ops[j]["eng"] is not None]

    count = {"V": 0, "S": 0, "P": 0, "G": 0}
    for o in issue:
        if o["dma"] is None and o["used"]:
            count[o["eng"]] += 1
            o["n"] = count[o["eng"]]
    waited = {}
    for o in issue:
        need = {}
        for d in o["deps"]:
            sem, val = d["ext"] if d["ext"] else ((d["dma"], 16) if d["dma"] else (d["eng"], d["n"]))
            need[sem] = max(need.get(sem, 0), val)
        for sem, val in need.items():
            if waited.get((o["eng"], sem), 0) < val:
                queue[o["eng"]].wait_ge(T.sem[sem], val)
                waited[(o["eng"], sem)] = val
        ins = o["fn"]()
        if o["dma"]:
            ins.then_inc(T.sem[o["dma"]], 16)
        elif o["used"]:
            ins.then_inc(T.sem[o["eng"]], 1)
    seen = {}
    for (eng, sem), val in waited.items():
        seen[sem] = max(seen.get(sem, 0), val)
    g.wait_ge(T.sem.sent, nsent[0])
    for o in issue:
        if o["dma"] and seen.get(o["dma"], 0) < 16:
            queue[o["eng"]].wait_ge(T.sem[o["dma"]], 16)
